import numpy as np, ml_dtypes
CORES = [24,25,26,27,28,29,30,31]
N = 8
BF = ml_dtypes.bfloat16
def gentries(a):
    return np.ascontiguousarray(a.reshape(8, 16, -1).transpose(0, 2, 1)).reshape(8, -1)
def gtable(e):
    e = np.asarray(e); return np.ascontiguousarray(e.reshape(8, -1, 16).transpose(0, 2, 1)).reshape(128, -1).astype(np.int32)
V, L, ST, RO, CAP = 1792, 256, 2, 2, 48
W = V + RO * ST * L
E = 4095
VOID = 2 ** 20
def pack(a, c, x, t, h):
    return {"a0": np.ascontiguousarray(a.reshape(N, 128, V)).astype(np.float32).astype(BF), "kids": np.ascontiguousarray(c.reshape(N, 128, V)).astype(np.int32),
            "x0": np.ascontiguousarray(x.reshape(N, 128, L)).astype(np.float32).astype(BF), "tops": np.stack([gtable(u) for u in t]), "th": np.ascontiguousarray(h).astype(np.int32)}
def near(rng, p, n):
    k = rng.integers(0, 24, (N, 8, 1, n)); z = rng.integers(1, 25, (N, 8, 1, n))
    v = np.take_along_axis(np.broadcast_to(p, (N, 8, 16, 24)), np.broadcast_to(k, (N, 8, 16, n)), 3)
    return np.clip(v + np.rint(z * rng.standard_normal((N, 8, 16, n))), 0, 255).astype(np.int64)
def parts(rng):
    p = rng.integers(0, 256, (8, 16, 24)); p[..., ::3] = rng.integers(0, 40, (8, 16, 8))
    fill = rng.choice(np.array([0.2, 0.5, 0.8, 1.0]), (N, 8, 1, V))
    c = np.where(rng.random((N, 8, 16, V)) < fill, rng.integers(0, V, (N, 8, 16, V)), E)
    hot = np.take_along_axis(rng.integers(0, V, (N, 8, 8)), rng.integers(0, 8, (N, 8, L)), 2)
    t = np.where(rng.random((N, 8, L)) < 0.2, hot, rng.integers(0, V, (N, 8, L)))
    h = np.minimum(rng.choice(np.array([60, 200, 500, 900, 4000]), (N, 8, L)) + rng.integers(0, 100, (N, 8, L)), 4080)
    return near(rng, p, V), c, near(rng, p, L), t, h
def setup_inputs(rng):
    return pack(*parts(rng))
def setup_inputs_spread(rng):
    a = np.minimum(np.exp2(8 * rng.random((N, 8, 1, V))) * rng.random((N, 8, 16, V)), 255).astype(np.int64)
    x = np.minimum(np.exp2(8 * rng.random((N, 8, 1, L))) * rng.random((N, 8, 16, L)), 255).astype(np.int64)
    fill = np.minimum(1.25 * rng.random((N, 8, 1, V)), 1.0)
    c = np.where(rng.random((N, 8, 16, V)) < fill, np.minimum((V * rng.random((N, 8, 16, V)) ** 2).astype(np.int64), V - 1), E)
    t = np.minimum((V * rng.random((N, 8, L)) ** 3).astype(np.int64), V - 1)
    h = np.minimum(np.exp2(12 * rng.random((N, 8, L))).astype(np.int64) - 1, 4080)
    return pack(a, c, x, t, h)
def setup_inputs_ends(rng):
    def both(n):
        k = rng.integers(0, 4, (N, 8, 1, n)); m = 255 * rng.integers(0, 2, (N, 8, 16, n))
        return np.where(k == 0, 0, np.where(k == 1, 255, m))
    a, x = both(V), both(L); a[..., 0] = 255 * rng.integers(0, 2, (N, 8, 16))
    h = 4080 * rng.integers(0, 2, (N, 8, L)); s = (N, 8, 16, V)
    c = np.where(rng.random(s) < 0.5, 0, np.where(rng.random(s) < 0.3, V - 1, rng.integers(0, V, s)))
    c = np.where(rng.random(s) < rng.choice(np.array([0.1, 0.4, 0.6, 1.0]), (N, 8, 1, V)), c, E)
    m = np.argsort(rng.random((N, 8, L)), axis=2) < (2 * L) // 3
    t = np.where(m, (V - 1) * rng.integers(0, 2, (N, 8, L)), rng.integers(1, V - 5, (N, 8, L)))
    t[:, 7] = np.where(m[:, 7], t[:, 7], rng.integers(1, V - 6 - (CAP + 2), (N, L)))
    a[..., V - 1] = 255; a[..., V - 2] = 255; c[..., V - 1] = E; c[..., V - 2] = E
    c[:, :, 2, V - 1] = V - 2; c[:, :, 15, V - 1] = V - 1; c[:, :, 15, V - 2] = V - 1
    a[..., V - 5] = 0; c[..., V - 5] = E; c[:, :, 0, V - 5] = V - 5; c[..., V - 4] = V - 5
    o = t[:, 1::2]; o[o == V - 1] = 0
    for q in range(N):
        i = np.nonzero(~m[q, 7, :L - 2])[0][-(CAP + 2):]; u = V - 6 - np.arange(CAP + 2)
        c[q, 7][:, u] = V - 5; x[q, 7][:, i] = 255; h[q, 7, i] = 0; t[q, 7, i] = u
    x[..., L - 1] = 0; h[..., L - 1] = 4080; t[..., L - 1] = V - 1
    x[..., L - 2] = 255; h[..., L - 2] = 0; t[..., L - 2] = V - 4
    return pack(a, c, x, t, h)
def setup_inputs_corners(rng):
    a = rng.integers(0, 201, (N, 8, 16, V)); x = rng.integers(201, 256, (N, 8, 16, L)); s = (N, 8, 16, V)
    c = np.where(rng.random(s) < rng.choice(np.array([0.1, 0.5, 0.9]), (N, 8, 1, V)), rng.integers(0, V, s), E)
    t = np.zeros((N, 8, L), np.int64); h = np.zeros((N, 8, L), np.int64)
    case = np.array([0, 1, CAP - 1, CAP, CAP + 1, L])[rng.integers(0, 6, (N, 8))]
    case[0] = (CAP, CAP + 1, L, CAP - 1, 1, 0, CAP, CAP + 1); case[1] = (0, L, 1, 0, CAP, CAP + 1, CAP - 1, 0); case[N - 1, 7] = CAP
    for q in range(N):
        for g in range(8):
            n = int(case[q, g]); o = rng.permutation(V); full, leaf, one, more = o[:L], o[L:L + 64], o[L + 64:L + 128], o[L + 128:]; k = c[q, g]
            k[:, full] = rng.integers(0, V, (16, L)); k[:, leaf] = E; k[:, one] = E; k[rng.integers(0, 16, 64), one] = rng.integers(0, V, 64)
            if n == 0: k[15, np.all(k == E, axis=0)] = V - 1
            w = rng.integers(0, 4, L); again = rng.choice(full[:n] if n else one, L)
            u = np.where(w == 0, again, np.where(w == 1, rng.choice(leaf, L), np.where(w == 2, rng.choice(one, L), rng.choice(more, L))))
            y = np.where((w == 0) & (n > 0), 0, 4080); i = rng.permutation(L)[:n]; u[i] = full[:n]; y[i] = 0
            t[q, g] = u; h[q, g] = y
    return pack(a, c, x, t, h)
def half(rng, who, n):
    return np.where(rng.random((16, n)) < 0.5, rng.choice(who, (16, n)), E)
def late(rng, A, C, X, T, H):
    u = rng.permutation(V)[:L // 2]; A[:] = rng.integers(0, 201, (16, V)); X[:] = rng.integers(201, 256, (16, L))
    C[:, u] = rng.integers(0, V, (16, L // 2)); C[rng.integers(0, 16, L // 2), u] = E
    T[:] = np.repeat(u, 2); H[:] = 0
def splits(rng, A, C, X, T, H):
    o = rng.permutation(V); s, b, d, far = o[:L], o[L:L + 16], o[L + 16:L + 32], o[L + 32:]
    A[:, far] = rng.integers(240, 256, (16, far.size)); A[:, b] = rng.integers(200, 211, (16, 16)); A[:, d] = rng.integers(100, 121, (16, 16))
    kb = rng.integers(0, 16, 16); kd = (kb + rng.integers(1, 16, 16)) & 15; w = rng.integers(0, 16, L)
    C[:] = E; C[:, far] = half(rng, far, far.size); C[:, b] = half(rng, far, 16); C[kb, b] = E; C[kd, b] = d
    C[:, s] = half(rng, far, L); C[kd[w], s] = rng.choice(far, L); C[kb[w], s] = b[w]
    X[:] = A[:, d[w]] + rng.integers(0, 3, (16, L)); T[:] = s; H[:] = rng.integers(400, 600, L)
def hosts(rng, A, C, X, T, H):
    o = rng.permutation(V); s, b, far = o[:L], o[L:2 * L], o[2 * L:]
    X[:] = rng.integers(100, 121, (16, L)); A[:, far] = rng.integers(240, 256, (16, far.size)); A[:, b] = X + rng.integers(5, 13, (16, L))
    C[:] = E; C[:, far] = half(rng, far, far.size); C[:, b] = half(rng, far, L); C[:, s] = half(rng, far, L); C[rng.integers(0, 16, L), s] = b
    T[:] = s; H[:] = rng.integers(900, 1100, L)
def made(rng, A, C, X, T, H):
    k = L // 8; o = rng.permutation(V); v, b, s, far = o[:k], o[k:2 * k], o[2 * k:3 * k], o[3 * k:]
    i = rng.permutation(L); pz = np.sort(i[:2 * k].reshape(k, 2), axis=1); p, z, r = pz[:, 0], pz[:, 1], i[2 * k:3 * k]
    n = rng.integers(12, 41, k); m = np.argsort(rng.random((16, k)), axis=0) < 8
    w = np.argsort(rng.random((16, k)), axis=0)[:3]; w[:2] = np.sort(w[:2], axis=0)
    A[:, far] = rng.integers(240, 256, (16, far.size)); A[:, b] = np.where(m, n, 0); A[:, s] = np.where(m, n, 2 * n)
    C[:] = E; C[:, far] = half(rng, far, far.size); C[w[0], v] = b; C[w[1], v] = s
    C[:, b] = rng.choice(far, (16, k)); C[w[2], b] = E
    T[:] = rng.choice(far, L); T[p] = v; T[z] = v; T[r] = b
    y = np.where(m, 2 * n, n); X[:, p] = y; X[:, z] = n; X[:, r] = y + rng.integers(1, 4, (16, k))
    H[p] = 12 * n; H[z] = 0; H[r] = 0
def setup_inputs_ties(rng):
    a = 100 * (rng.random((N, 8, 1, V)) < 0.6) + rng.integers(0, 3, (N, 8, 16, V)) * (rng.random((N, 8, 1, V)) < 0.8)
    x = 100 + rng.integers(0, 3, (N, 8, 16, L)) * (rng.random((N, 8, 1, L)) < 0.8); s = (N, 8, 16, V)
    c = np.where(rng.random(s) < 0.5, rng.integers(0, 64, s), rng.integers(0, V, s))
    c = np.where(rng.random(s) < rng.choice(np.array([0.2, 0.6, 0.9, 1.0]), (N, 8, 1, V)), c, E)
    h = np.where(rng.random((N, 8, L)) < 0.8, rng.integers(0, 20, (N, 8, L)), 1600)
    t = rng.integers(0, V, (N, 8, L))
    for q in range(N):
        for g, fn in ((1, late), (2, splits), (4, hosts), (6, made)):
            if g == 1 or q % 2 == 0: fn(rng, a[q, g], c[q, g], x[q, g], t[q, g], h[q, g])
    return pack(a, c, x, t, h)
def setup_inputs_alike(rng):
    a, c, x, t, h = parts(rng)
    c[:, 0] = rng.integers(0, V, (N, 1, V)); c[:, 1] = np.where(c[:, 1] == E, E, np.arange(V))
    t[:, 2] = rng.integers(0, V, (N, 1)); t[:, 3] = np.where(rng.random((N, L)) < 0.5, rng.integers(0, V, (N, 1)), V - 1)
    c[:, 4] = np.where(c[:, 4] == E, E, rng.choice(np.array([0, 5, V - 1]), (N, 16, V)))
    a[:, 5] = np.minimum(a[:, 5], 200); c[:, 5] = rng.integers(0, V, (N, 16, V)); t[:, 5] = np.arange(L) % CAP
    x[:, 5] = rng.integers(201, 256, (N, 16, L)); h[:, 5] = 0
    x[:, 6] = x[:, 6, :, :1]
    c[:, 7] = rng.integers(0, V, (N, 16, V))
    return pack(a, c, x, t, h)
def check_inputs(d):
    bad = []
    for k, lo, hi in (("a0", 0, 255), ("kids", 0, E), ("x0", 0, 255), ("tops", 0, V - 1), ("th", 0, 4080)):
        v = np.asarray(d[k]).astype(np.float64)
        if not (np.min(v) >= lo and np.max(v) <= hi) or np.any(v != np.floor(v)): bad.append("range of " + k)
        elif k == "kids" and np.any((v >= V) & (v != E)): bad.append("range of " + k)
    return bad
def first(key, on):
    k = np.where(on, key, 8192 + np.arange(L)); o = np.argsort(k, axis=1, kind="stable"); s = np.take_along_axis(k, o, 1)
    m = np.ones(k.shape, bool); m[:, 1:] = s[:, 1:] != s[:, :-1]
    r = np.zeros(k.shape, bool); np.put_along_axis(r, o, m, 1)
    return r & on
def pick(t, i):
    return t[np.arange(t.shape[0]).reshape((-1,) + (1,) * (i.ndim - 1)), i]
def at(t, k):
    return np.take_along_axis(t, k[..., None], 2)[..., 0]
def reference(a0, kids, x0, tops, th):
    B = 8 * N
    A = np.zeros((B, W, 16), np.int32); A[:, :V] = a0.astype(np.float32).astype(np.int32).reshape(B, 16, V).transpose(0, 2, 1)
    C = np.full((B, W, 16), E, np.int32); C[:, :V] = kids.reshape(B, 16, V).transpose(0, 2, 1)
    x = np.ascontiguousarray(x0.astype(np.float32).astype(np.int32).reshape(B, 16, L).transpose(0, 2, 1))
    top = np.stack([gentries(u) for u in tops]).astype(np.int64).reshape(B, L); lim = th.reshape(B, L).astype(np.int32)
    for rnd in range(RO):
        v = top.copy(); rest = np.zeros((B, L), bool)
        come = np.zeros((N, 8, ST * CAP, 16), np.int32); ok = np.zeros((N, 8, ST * CAP), bool)
        for j in range(ST):
            sg = rnd * ST + j; act = first(v, ~rest)
            c = pick(C, v); filled = c != E
            e = np.where(filled, np.add.reduce(np.abs(x[:, :, None] - pick(A, np.where(filled, c, 0))), axis=3), VOID)
            kb = np.argmin(e, axis=2); eb = at(e, kb); e2 = e.copy(); np.put_along_axis(e2, kb[..., None], VOID, 2)
            kq = np.argmin(e2, axis=2); eq = at(e2, kq)
            b = np.where(eb < VOID, at(c, kb), 0); q = np.where(eq < VOID, at(c, kq), 0)
            ab = pick(A, b); mid = (ab + pick(A, q)) >> 1
            em = np.where(eq < VOID, np.add.reduce(np.abs(x - mid), axis=2), VOID)
            d = np.where((eb < VOID)[..., None], pick(C, b), E)
            f = np.where(d != E, np.add.reduce(np.abs(x[:, :, None] - pick(A, np.where(d != E, d, 0))), axis=3), VOID)
            w = np.argmin(np.stack([eb, em, np.min(f, axis=2), lim], axis=2), axis=2)
            host, merge, split, new = [act & (w == u) for u in range(4)]
            empty = ~filled; room = np.any(empty, axis=2); k0 = np.argmax(empty, axis=2); over = new & ~room
            n = V + L * sg + np.arange(L)
            g, i = np.nonzero(host & first(b, host))
            A[g, b[g, i]] = ab[g, i] + np.clip(x[g, i] - ab[g, i], -4, 4)
            g, i = np.nonzero(merge)
            A[g, n[i]] = mid[g, i]; C[g, n[i], kb[g, i]] = b[g, i]; C[g, n[i], kq[g, i]] = q[g, i]
            C[g, v[g, i], kb[g, i]] = n[i]; C[g, v[g, i], kq[g, i]] = E
            g, i = np.nonzero(split)
            t = c[g, i]; t[np.arange(len(g)), kb[g, i]] = E; C[g, v[g, i]] = np.where(t == E, d[g, i], t)
            g, i = np.nonzero(new & room)
            A[g, n[i]] = x[g, i]; C[g, v[g, i], k0[g, i]] = n[i]
            v = np.where(host, b, np.where(merge, n, v)); rest = rest | new
            pl = np.add.accumulate(over.astype(np.int64), axis=1) - 1; g, i = np.nonzero(over & (pl < CAP))
            to = (g // 8 + 1 + sg % (N - 1)) % N
            come[to, g % 8, j * CAP + pl[g, i]] = x[g, i]; ok[to, g % 8, j * CAP + pl[g, i]] = True
        ok = ok.reshape(B, ST * CAP); come = pick(come.reshape(B, ST * CAP, 16), np.argsort(~ok, axis=1, kind="stable"))
        cnt = np.add.reduce(ok.astype(np.int64), axis=1)[:, None]; nr = np.add.accumulate(rest.astype(np.int64), axis=1) - 1
        got = rest & (nr < cnt)
        x = np.where(got[..., None], pick(come, np.clip(nr, 0, ST * CAP - 1)), np.abs(x - pick(A, v)))
    return {"ya": np.ascontiguousarray(A.transpose(0, 2, 1)).reshape(N, 128, W).astype(np.float32).astype(BF),
            "yc": np.ascontiguousarray(C.transpose(0, 2, 1)).reshape(N, 128, W).astype(np.float32),
            "yx": np.ascontiguousarray(x.transpose(0, 2, 1)).reshape(N, 128, L).astype(np.float32).astype(BF)}

@@ -1,0 +1,662 @@
+from concourse.mybir import dt, AluOpType, AxisListType, ActivationFunctionType
+
+OP = AluOpType
+FN = ActivationFunctionType
+F, B, I, U = "float32", "bfloat16", "int32", "uint16"
+SHAPES = {
+    "kint": (1792, I), "kw": (4608, F), "aw": (4352, B), "xe": (4096, B),
+    "xb": (768, B), "xw0": (384, B), "xw1": (384, B), "sb": (2112, B),
+    "cu": (256, U), "du": (256, U), "kc": (256, F), "idp": (256, F), "y0": (256, F),
+    "df": (4096, B), "df2": (4096, B), "ga": (2048, B), "e0": (256, B), "oh0": (256, B),
+    "msk": (264, F), "eq": (256, F), "cn": (256, F), "zz": (256, F), "zs": (256, F), "cs": (256, F),
+    "es": (256, F), "zi": (16, I), "bi": (16, I), "bu": (16, U), "ki": (32, I), "kk": (32, I), "lb": (32, F), "lbu": (32, U),
+    "kh": (16, I), "w0": (16, F), "w1": (16, F), "w2": (16, F), "w3": (16, I), "typ": (16, I),
+    "dbh": (256, F), "db": (256, B), "sq": (256, F), "mg": (256, F), "am": (256, B), "c4": (256, B), "candw": (528, B),
+    "src": (96, F), "ct": (160, F), "mt": (144, F), "ut": (128, F), "st1": (64, F), "st": (64, F), "su": (64, U), "dft": (144, F),
+    "mxr": (256, F), "zr": (256, F), "er": (256, F), "fe": (256, F),
+    "codel": (256, B), "coder": (256, B), "cnt": (16, F), "aj": (256, B), "thr": (32, F), "bs": (32, F),
+    "hf": (32, F), "u3": (32, F), "s3": (32, F), "tsu": (32, U), "av": (256, B), "xdt": (256, B),
+    "tmp": (160, F), "ov": (16, B), "restb": (16, B), "rest": (16, F), "nrest": (16, F), "nrx": (16, F),
+    "gate": (32, F), "scu": (32, U), "ruf": (16, F), "ru": (16, U), "vup": (16, U), "posu": (16, U), "bcl": (16, U),
+    "kn": (16, F), "yt": (2816, F),
+    "ip": (4, I), "rg": (10, F), "k16": (16, F), "jc": (128, F), "njb": (16, B), "wide": (256, F), "wt": (1024, B), "sq1": (768, F),
+    "sr": (2064, B), "pm": (512, F), "wb": (896, B), "rst": (128, F), "rz": (128, F),
+    "mxt": (288, B), "knt": (288, B), "code": (2832, B), "fl": (16, F), "constr": (256, B), "constl": (256, B),
+    "rc": (16, F), "repc": (10, U), "repu": (10, U), "types": (144, F), "nu": (1024, F), "thp": (256, I), "thq": (512, I), "thb": (512, B),
+    "tl": (16, I), "tf": (16, F), "tu": (16, U), "tup": (16, U), "kr": (160, B),
+}
+SCRATCH = {n: ("sbuf", [128, w], d) for n, (w, d) in SHAPES.items()}
+SCRATCH["dx"] = ("sbuf", [128, 16, 16, 16], B)
+SCRATCH["y4"] = ("sbuf", [128, 8, 2, 16], F)
+SCRATCH["bd"] = ("sbuf", [128, 16, 128], B)
+for _n in range(8):
+    SCRATCH["ps%d" % _n] = ("psum", [128, 512], F)
+SEMAPHORES = ["qv", "qa", "qp", "qg", "lth", "bdw", "snt", "out", "outa"] + ["l%d" % n for n in range(6)] + ["arr%d" % n for n in range(4)]
+BIG = 1.0e9
+MAGIC = 12582912.0
+VOIDA = 16384.0
+A_ = slice(None)
+
+
+def R(name, lo=0, hi=None, step=1):
+    hi = (SHAPES[name][0] if name in SHAPES else 512) if hi is None else hi
+    return ("r", name, (A_, slice(lo, hi) if step == 1 else slice(lo, hi, step)), lo, hi)
+
+
+def RX(name, idx, lo, hi):
+    return ("r", name, idx, lo, hi)
+
+
+def IND(win, off):
+    return ("i", win, off)
+
+
+def emitter(g, T):
+    q = {"v": g.vector, "a": g.scalar, "p": g.tensor, "s": g.sync, "g": g}
+    own = {"v": "qv", "a": "qa", "p": "qp", "g": "qg"}
+    count, known, snap, wr, rd, bank = {}, {k: {} for k in q}, {}, {}, {}, {}
+
+    def ap(x):
+        if x[0] == "i":
+            return T[x[1][1]][x[1][2]].indirect(T[x[2][1]][x[2][2]])
+        return T[x[1]][x[2]]
+
+    def need(k, outs, ins):
+        d = {}
+
+        def add(tag):
+            d[tag[0]] = max(d.get(tag[0], 0), tag[1])
+        for x in ins + outs:
+            if x[1][:2] == "ps":
+                for k2, tag in bank.get(x[1], {}).items():
+                    if k2 != k:
+                        add(tag)
+        for x in ins:
+            for lo, hi, tag, k2 in wr.get(x[1], []):
+                if lo < x[4] and x[3] < hi and x[1][:2] != "ps":
+                    add(tag)
+        for x in outs:
+            if x[1][:2] == "ps":
+                continue
+            for lst in (wr, rd):
+                for lo, hi, tag, k2 in lst.get(x[1], []):
+                    if lo < x[4] and x[3] < hi:
+                        add(tag)
+        return d
+
+    def wait(k, d):
+        for s, v in sorted(d.items(), key=lambda z: -len(snap.get(z, {}))):
+            if known[k].get(s, 0) < v:
+                q[k].wait_ge(T.sem[s], v)
+                known[k][s] = v
+                for s2, v2 in snap.get((s, v), {}).items():
+                    known[k][s2] = max(known[k].get(s2, 0), v2)
+
+    def note(k, outs, ins, tag):
+        snap[tag] = dict(known[k])
+        for x in outs:
+            if x[1][:2] == "ps":
+                bank.setdefault(x[1], {})[k] = tag
+                continue
+            for lst in (wr, rd):
+                lst[x[1]] = [e for e in lst.get(x[1], []) if not (x[3] <= e[0] and e[1] <= x[4])]
+            wr[x[1]].append((x[3], x[4], tag, k))
+        for x in ins:
+            if x[1][:2] == "ps":
+                bank.setdefault(x[1], {})[k] = tag
+                continue
+            lst = [e for e in rd.get(x[1], []) if not (e[3] == k and x[3] <= e[0] and e[1] <= x[4] and e[2][0] == tag[0])]
+            lst.append((x[3], x[4], tag, k))
+            rd[x[1]] = lst
+
+    def flat(xs):
+        r = []
+        for x in xs:
+            if isinstance(x, tuple):
+                r += [x[1], x[2]] if x[0] == "i" else [x]
+        return r
+
+    def op(k, call, out, ins, more=()):
+        outs = [out[1]] if out[0] == "i" else [out]
+        i2 = flat(ins) + ([out[2]] if out[0] == "i" else [])
+        outs += flat(more)
+        wait(k, need(k, outs, i2))
+        s = own[k]
+        count[s] = count.get(s, 0) + 1
+        call().then_inc(T.sem[s], 1)
+        note(k, outs, i2, (s, count[s]))
+
+    def val(x):
+        return ap(x) if isinstance(x, tuple) else x
+
+    e = {}
+    e["tt"] = lambda o, a, b, f: op("v", lambda: g.vector.tensor_tensor(ap(o), ap(a), ap(b), f), o, [a, b])
+
+    def ts(o, a, s1, f1, s2=None, f2=None):
+        if f2 is None:
+            op("v", lambda: g.vector.tensor_scalar(ap(o), ap(a), val(s1), None, f1), o, [a, s1])
+        else:
+            op("v", lambda: g.vector.tensor_scalar(ap(o), ap(a), val(s1), val(s2), f1, f2), o, [a, s1, s2])
+    e["ts"] = ts
+    e["tc"] = lambda o, a: op("v", lambda: g.vector.tensor_copy(ap(o), ap(a)), o, [a])
+    e["ms"] = lambda o, c: op("v", lambda: g.vector.memset(ap(o), c), o, [])
+    e["scan"] = lambda o, a, b, c, f1, f2: op("v", lambda: g.vector.tensor_tensor_scan(ap(o), ap(a), ap(b), c, f1, f2), o, [a, b])
+    e["tr"] = lambda o, a: op("v", lambda: g.vector.transpose(ap(o), ap(a)), o, [a])
+    e["red"] = lambda o, a, f: op("v", lambda: g.vector.tensor_reduce(ap(o), ap(a), AxisListType.X, f), o, [a])
+
+    def act(o, a, f, bias=0.0, scale=1.0, acc=None):
+        if acc is not None:
+            op("a", lambda: g.scalar.activation(ap(o), ap(a), f, accum_out=ap(acc)), o, [a], [acc])
+        elif f == FN.Copy:
+            op("a", lambda: g.scalar.activation(ap(o), ap(a), f), o, [a])
+        else:
+            op("a", lambda: g.scalar.activation(ap(o), ap(a), f, bias=val(bias), scale=val(scale)), o, [a, bias, scale])
+    e["act"] = act
+    e["mm"] = lambda o, l, r, s0, s1: op("p", lambda: g.tensor.matmul(ap(o), ap(l), ap(r), s0, s1), o, [l, r])
+    e["iota"] = lambda o, pat, base, cm: op("g", lambda: g.iota(ap(o), pat, base, cm, allow_small_or_imprecise_dtypes=True), o, [])
+    e["aff"] = lambda o, a, pat, f, fill, base, cm: op("g", lambda: g.affine_select(ap(o), ap(a), pat, f, fill, base, cm), o, [a])
+
+    def dma(k, o, a, sem, src=None, dst=None):
+        outs, ins = ([] if o is None else [o]), ([] if a is None else [a])
+        wait(k, need("s", outs, ins))
+        count[sem] = count.get(sem, 0) + 16
+        q[k].dma_start(dst if o is None else ap(o), src if a is None else ap(a)).then_inc(T.sem[sem], 16)
+        v = count[sem] if sem[0] == "l" and sem != "lth" else -(-count[sem] // 128) * 128
+        note("s", outs, ins, (sem, v))
+    e["dma"] = dma
+
+    def remote(o, a, sem, rid, pid, mask, n):
+        wait("g", need("s", [], [a]))
+        count["snt"] = count.get("snt", 0) + n
+        g.remote_dma(ap(o), ap(a), T.sem[sem], T.sem.snt, pid, rid, mask)
+        count[sem] = n
+
+    def landed(o, sem):
+        note("s", [o], [], (sem, count[sem]))
+    e["remote"], e["landed"] = remote, landed
+
+    def finish():
+        for s, v in count.items():
+            q["s"].wait_ge(T.sem[s], v)
+    e["finish"] = finish
+    return e
+
+
+def rank_program(g, core, T, topo):
+    rank = T.rank_of(core)
+    if rank is None:
+        return
+    e = emitter(g, T)
+    tt, ts, tc, ms, scan, tr, red, act, mm, iota, aff, dma = [e[n] for n in ("tt", "ts", "tc", "ms", "scan", "tr", "red", "act", "mm", "iota", "aff", "dma")]
+    add, sub, mul, mx, mn, eqq, lt, le, ge = OP.add, OP.subtract, OP.mult, OP.max, OP.min, OP.is_equal, OP.is_lt, OP.is_le, OP.is_ge
+    Id, Cp, Ab, Re = FN.Identity, FN.Copy, FN.Abs, FN.Relu
+    tmp = lambda n: R("tmp", 16 * n, 16 * n + 16)
+    sq1 = lambda n: R("sq1", 128 * n, 128 * n + 128)
+    BDALL = RX("bd", (A_, A_, A_), 0, 2048)
+
+    dma("s", R("tl"), None, "l0", src=T.tops[:])
+    ms(R("thp"), 0)
+    dma("s", R("kint", 0, 896), None, "l2", src=T.kids[:, 0:896])
+    dma("a", R("kint", 896, 1792), None, "l3", src=T.kids[:, 896:1792])
+    dma("s", R("xb", 0, 256), None, "l1", src=T.x0[:])
+    for n in range(8):
+        dma("s", RX("thp", (slice(16 * n, 16 * n + 1), A_), 32 * n, 32 * n + 32), None, "lth", src=T.th[n:n + 1, :])
+    dma("s", R("aw", 0, 896), None, "l4", src=T.a0[:, 0:896])
+    dma("a", R("aw", 896, 1792), None, "l5", src=T.a0[:, 896:1792])
+    ms(sq1(0), 1.0)
+    ms(R("kw", 1792, 2816), 0.0)
+    ms(R("aw", 1792, 2816), 0.0)
+    ms(R("sr"), 0.0)
+    iota(R("ip", 0, 1), [[1, 1]], 0, 1)
+    iota(R("k16"), [[1, 16]], 0, 0)
+    iota(R("jc", 0, 16), [[16, 16]], 0, 0)
+    iota(R("aw", 2816, 4096), [[0, 1280]], int(VOIDA), 0)
+    iota(R("kw", 2816, 4096), [[0, 1280]], 0, 0)
+    aff(sq1(1), sq1(0), [[-1, 128]], eqq, 0.0, 0, 1)
+    aff(sq1(2), sq1(0), [[-1, 128]], eqq, 0.0, 16, 1)
+    aff(sq1(3), sq1(0), [[-1, 128]], eqq, 0.0, -16, 1)
+    iota(R("kr", 0, 64), [[0, 4], [1, 16]], 0, 0)
+    iota(R("kr", 64, 128), [[0, 64]], 2, 0)
+    iota(R("kr", 128, 144), [[0, 16]], 1, 0)
+    iota(R("kr", 144, 160), [[0, 16]], 3, 0)
+    aff(sq1(4), sq1(0), [[-16, 8], [0, 16]], ge, 0.0, 0, 1)
+    aff(sq1(4), sq1(4), [[16, 8], [0, 16]], ge, 0.0, 15, -1)
+    aff(sq1(5), sq1(4), [[1, 128]], OP.is_gt, 0.0, 0, -1)
+    iota(R("nu", 0, 256), [[1, 256]], 1792 - 4095, 0)
+    iota(BDALL, [[0, 2048]], 0, 0)
+    iota(R("wide"), [[1, 256]], 0, 0)
+    for n, v in enumerate((0, 5, 2, 1, 3, 0, 0, 4, 0)):
+        iota(R("rc", n, n + 1), [[0, 1]], 16 * v, 0)
+    for n, v in enumerate((2, 9, 1, 2, 3, 0, 0, 1, 5)):
+        iota(R("types", 16 * n, 16 * n + 16), [[0, 16]], v, 0)
+    for n, v in enumerate((4095, 2816, None, 272, 4095, 2816, None, 272)):
+        if v:
+            iota(R("dft", 16 * n, 16 * n + 16), [[0, 16]], v, 0)
+    iota(R("src", 80, 96), [[0, 16]], 0, 0)
+    iota(R("wt", 0, 256), [[1, 16], [0, 16]], 0, 0)
+    iota(R("wt", 256, 512), [[0, 16], [1, 16]], 0, 0)
+    iota(R("candw", 0, 16), [[0, 16]], 0, 0)
+    for n in range(4):
+        iota(R("sb", 528 * n, 528 * n + 64), [[0, 64]], 0, 0)
+    for n in (1, 2, 3):
+        iota(R("nu", 256 * n, 256 * n + 256), [[1, 256]], 1792 - 4095 + 256 * n, 0)
+
+    ri, gi, oi = R("ip", 1, 2), R("ip", 2, 3), R("ip", 3, 4)
+    ts(ri, R("ip", 0, 1), 15, OP.bitwise_and)
+    ts(gi, R("ip", 0, 1), 4, OP.arith_shift_right)
+    ts(oi, gi, 1, OP.bitwise_and)
+    rf, gf, odd, even, bk, m1, m2, m3, fz, is12 = [R("rg", n, n + 1) for n in range(10)]
+    tc(rf, ri)
+    tc(gf, gi)
+    tc(odd, oi)
+    act(even, odd, Id, bias=1.0, scale=-1.0)
+    act(bk, rf, Id, bias=4095.0, scale=4096.0)
+    tc(R("tu"), R("tl"))
+    tc(R("tf"), R("tl"))
+    tc(R("tup", 0, 16, 2), R("tu", 0, 8))
+    tc(R("tup", 1, 16, 2), R("tu", 8, 16))
+    ts(R("code", 0, 1), rf, 12.0, lt, -1.0, mul)
+    ts(R("fl"), R("k16"), rf, eqq, -2.0, mul)
+    act(R("fl"), R("fl"), Id, bias=1.0)
+    for b in range(12):
+        n, w = 1 << b, min(1 << b, 2816 - (1 << b))
+        act(R("code", n, n + w), R("code", 0, w), Id, scale=R("fl", b, b + 1))
+    ms(R("code", 2816, 2832), 0.0)
+    b8 = R("tmp", 0, 8)
+    ts(b8, R("k16", 0, 8), gf, eqq, 16.0, mul)
+    ms(tmp(1), 1.0)
+    for n in range(8):
+        ts(RX("sr", (A_, slice(16 * n, 16 * n + 129 * 15 + 1, 129)), 0, 2064), tmp(1), R("tmp", n, n + 1), mul)
+    wones, ident, nident, l0, bm, lp, m4i = [R("wb", 128 * n, 128 * n + 128) for n in range(7)]
+    ms(wones, 1.0 / 128)
+    ms(R("rst"), -BIG)
+    ms(R("rst", 0, 128, 16), BIG)
+    ms(R("rz"), 1.0)
+    ms(R("rz", 0, 128, 16), 0.0)
+    ms(R("msk", 0, 8), 0.0)
+    ms(R("nrest"), 0.0)
+    jt, jd96, jd52, j16p, j272, jn272, j16, _j7 = [R("jc", 16 * n, 16 * n + 16) for n in range(8)]
+    ts(jt, jt, rf, add)
+    for n, src, s in ((0, sq1(1), even), (1, sq1(2), even), (2, sq1(3), odd), (3, sq1(1), odd)):
+        act(R("pm", 128 * n, 128 * n + 128), src, Id, scale=s)
+    for o, c, m in ((jd96, 4096.0, 1.0), (jd52, 4352.0, 1.0), (j16p, 16.0, 1.0), (j272, 272.0, 1.0), (jn272, 272.0, -1.0), (j16, 0.0, 16.0),
+                    (R("njb"), 0.0, -1.0), (R("src", 48, 64), 4096.0, 1.0), (R("dft", 128, 144), 4096.0, 1.0), (R("ct", 144, 160), 16.0, 1.0)):
+        act(o, jt, Id, bias=c, scale=m)
+    act(ident, sq1(1), Cp)
+    act(nident, sq1(1), Id, scale=-1.0)
+    act(m4i, sq1(1), Id, scale=-4096.0)
+    ts(R("kw", 0, 896), R("kint", 0, 896), -4095.0, add)
+    ts(R("kw", 896, 1792), R("kint", 896, 1792), -4095.0, add)
+
+    def thresholds():
+        ts(R("thq", 0, 256), R("thp"), 63, OP.bitwise_and)
+        ts(R("thq", 256, 512), R("thp"), 4032, OP.bitwise_and)
+        tc(R("thb"), R("thq"))
+
+    def xx(p):
+        return R("xb", 256 * p, 256 * p + 256)
+
+    def expand_x(xb):
+        for k in range(16):
+            o = RX("xe", (A_, slice(k, 4096, 16)), 256 * k, 256 * k + 256)
+            if k % 3:
+                tc(o, xb)
+            else:
+                act(o, xb, Cp)
+
+    def constants_2():
+        tt(l0, sq1(1), sq1(5), sub)
+        act(bm, sq1(4), Cp)
+        tt(lp, sq1(5), sq1(4), sub)
+        ts(R("repu"), R("k16", 0, 10), 0.0, mul, rf, add)
+        ts(R("repc", 0, 9), R("rc", 0, 9), rf, add)
+        tc(R("dft", 32, 48), R("tf"))
+        tc(R("dft", 96, 112), R("tf"))
+        a, b, c = R("tmp", 32, 33), R("tmp", 33, 34), R("tmp", 34, 35)
+        ts(is12, rf, 12.0, eqq)
+        ts(b, rf, 13.0, eqq)
+        ts(c, rf, 14.0, eqq)
+        act(m1, b, Id, scale=-1.0 / 256)
+        act(m2, is12, Id, scale=1.0 / 256)
+        act(a, c, Id, scale=-12.0)
+        tt(m2, m2, a, add)
+        tt(m3, b, c, add)
+        act(R("constr"), R("wide"), Id, bias=m2, scale=m1)
+        act(R("constl"), R("wide"), Id, bias=m3, scale=is12)
+        for n in range(8):
+            p = slice(16 * n + 12, 16 * n + 16)
+            dma("s", RX("bd", (p, A_, slice(16 * n, 16 * n + 16)), 256 * n, 256 * n + 256), RX("constl", (p, A_), 0, 256), "bdw")
+
+    def constants_3():
+        eb, ek = R("wt", 512, 768), R("wt", 768, 1024)
+        ts(eb, R("wt", 0, 256), rf, eqq)
+        ts(ek, R("wt", 256, 512), rf, eqq)
+        ps = R("ps3", 128, 384)
+        mm(ps, ident, eb, True, False)
+        mm(ps, ident, ek, False, True)
+        act(R("knt", 0, 256), ps, Cp)
+        mm(ps, m4i, eb, True, False)
+        mm(ps, m4i, ek, False, False)
+        mm(ps, ident, eb, False, True)
+        act(R("mxt", 0, 256), ps, Id, bias=4096.0)
+        ms(R("knt", 256, 288), 0.0)
+        ms(R("mxt", 272, 288), 4096.0)
+        ts(tmp(2), R("k16"), rf, eqq)
+        act(R("mxt", 256, 272), tmp(2), Id, bias=4096.0, scale=-4096.0)
+        for h in (0, 256):
+            for r in range(16):
+                mm(R("ps3", 32, 48), sr(r), R("thb", h + r, h + 256, 16), h == 0 and r == 0, False)
+        mm(R("ps3", 32, 48), wones, R("kr", 144, 160), False, True)
+        act(R("kn"), R("ps3", 32, 48), Cp)
+
+    def sr(r):
+        return R("sr", 128 * r, 128 * r + 128)
+
+    DB = {15: ("ps4", 0), 14: ("ps4", 256), 13: ("ps5", 0), 12: ("ps5", 224), 3: ("ps5", 432), 4: ("ps3", 256), 2: ("ps3", 336), 1: ("ps3", 384), 0: ("ps3", 416),
+          11: ("ps6", 0), 10: ("ps6", 192), 7: ("ps6", 368), 9: ("ps7", 0), 8: ("ps7", 160), 6: ("ps7", 304), 5: ("ps7", 416)}
+    DV, DA = (15, 14, 13, 12, 3, 4, 2, 1, 0), (11, 10, 7, 9, 8, 6, 5)
+
+    def dd_left(lu):
+        act(R("codel"), IND(R("code"), lu), Cp)
+        for n in range(8):
+            p = slice(16 * n, 16 * n + 12)
+            dma("s", RX("bd", (p, A_, slice(16 * n, 16 * n + 16)), 256 * n, 256 * n + 256), RX("codel", (p, A_), 0, 256), "bdw")
+
+    def dd_right(ru):
+        tt(R("coder"), IND(R("code"), ru), R("constr"), add)
+
+    def dd_out(c):
+        n, o = DB[c]
+        return R(n, o, o + 16 * c + 16)
+
+    def dd_mm(cs):
+        for c in cs:
+            mm(dd_out(c), RX("bd", (A_, c, A_), 0, 2048), R("coder", 0, 16 * c + 16), True, True)
+
+    def dd_red(c, v):
+        if v:
+            red(R("cnt", c, c + 1), dd_out(c), mx)
+        else:
+            act(R("aj", 0, 16 * c + 16), dd_out(c), Re, acc=R("cnt", c, c + 1))
+
+    def acting(t):
+        a, b = tmp(4), tmp(5)
+        tt(b, R("dft", 32, 48), jd52, sub)
+        tt(a, R("cnt"), R("nrest"), le)
+        act(R("gate", 16 * t, 16 * t + 16), a, Id, scale=1.0e6, bias=-12.0)
+        tt(b, a, b, mul)
+        tt(b, b, jd52, add)
+        tc(R("scu", 16 * t, 16 * t + 16), b)
+
+    def chunk(q, dst, lst, krow, act_gather=None):
+        lists = R(lst, 64 * q, 64 * q + 64)
+        dxo = lambda a, b: RX("dx", (A_, slice(a, b), A_, A_), 256 * a, 256 * b)
+        if act_gather:
+            for h, bk2 in enumerate(act_gather):
+                act(dxo(4 * q + 2 * h, 4 * q + 2 * h + 2), R(bk2), Ab)
+        else:
+            o = R(dst, 1024 * q, 1024 * q + 1024)
+            tt(o, IND(R("aw", 0, 4096), lists), RX("xe", (A_, slice(1024 * q, 1024 * q + 1024)), 0, 4096), sub)
+            act(dxo(4 * q, 4 * q + 4), o, Ab)
+        n, lo = ("ps0", "ps1")[q // 2], 64 * (q % 2)
+        out = R(n, lo, lo + 64)
+        mm(out, wones, krow, True, False)
+        for r in range(16):
+            mm(out, sr(r), RX("dx", (A_, slice(4 * q, 4 * q + 4), r, A_), 1024 * q, 1024 * q + 1024), False, r == 15)
+
+    def gather_ahead(q, lst, n0, b1, b2):
+        act(R("ga", n0, n0 + 1024), IND(R("aw", 0, 4096), R(lst, 64 * q, 64 * q + 64)), Cp)
+        for h, bk2 in ((0, b1), (1, b2)):
+            mm(R(bk2), nident, RX("xe", (A_, slice(1024 * q + 512 * h, 1024 * q + 512 * h + 512)), 0, 4096), True, False)
+            mm(R(bk2), ident, R("ga", n0 + 512 * h, n0 + 512 * h + 512), False, True)
+
+    def best(h):
+        key = R(("ps0", "ps1")[h], 0, 128)
+        w = lambda n: R(n, 128 * h, 128 * h + 128)
+        tile = lambda n: R(n, 8 * h, 8 * h + 8)
+        m = lambda d: R("msk", 128 * h + d, 128 * h + 128 + d)
+        scan(m(8), R("rst"), key, BIG, mx, mn)
+        tt(w("eq"), m(8), key, eqq)
+        tt(w("cn"), m(7), key, mx)
+        tt(w("zz"), w("eq"), R("ps2", 128 * h, 128 * h + 128), mul)
+        scan(w("zs"), R("rz"), w("zz"), 0.0, mul, mx)
+        tc(tile("zi"), R("zs", 128 * h + 15, 128 * h + 128, 16))
+        scan(w("cs"), w("cn"), R("rst"), BIG, mn, mx)
+        ts(tile("bi"), tile("zi"), 4095, OP.bitwise_and)
+        tc(tile("bu"), tile("bi"))
+        ts(w("du"), IND(R("kw", 0, 4096), tile("bu")), 4095.0, add)
+
+    def head(t, n0):
+        vu, vup = (R("tu"), R("tup")) if t == 0 else (R("su", 32, 48), R("vup"))
+        act(R("idp"), IND(R("kw", 0, 4096), vup), Id, bias=bk)
+        ts(R("cu"), IND(R("kw", 0, 4096), vu), 4095.0, add)
+        act(R("kc"), IND(R("kw", 0, 4096), vu), Cp)
+        act(R("src", 32, 48), jt, Id, bias=float(n0))
+        mm(R("ps0", 128, 384), sq1(1), R("kc"), True, True)
+
+    def head_ids():
+        tr(R("y0"), R("idp"))
+        act(RX("y4", (A_, A_, A_, A_), 0, 256), R("y0"), Cp)
+        for cc in (0, 1):
+            for gg in (0, 1):
+                mm(R("ps2", 128 * cc, 128 * cc + 128), R("pm", 256 * cc + 128 * gg, 256 * cc + 128 * gg + 128), RX("y4", (A_, A_, gg, A_), 0, 256), gg == 0, gg == 1)
+
+    def step(p, t):
+        s = 2 * p + t
+        xb, vt = xx(p), R("dft", 32, 48)
+        vu = R("tu") if t == 0 else R("su", 32, 48)
+        n0 = 1792 + 256 * s
+        nu = R("nu", 256 * s, 256 * s + 256)
+        ded = t == 1 or s == 0
+        krow, two = R("kr", 0, 64), R("kr", 64, 128)
+        kcp = R("ps0", 128, 384)
+        chunk(0, "df", "cu", krow)
+        if s == 0:
+            constants_2()
+        if t == 1:
+            tt(R("ruf"), R("ruf"), R("rest"), mul)
+            tt(R("ruf"), R("ruf"), vt, add)
+            tc(R("ru"), R("ruf"))
+            prefix_mm(R("ov"), -256.0)
+        act(R("e0"), R("kc"), Re, bias=1.0)
+        chunk(1, "df", "cu", krow)
+        if ded:
+            dd_left(vu)
+            dd_right(vu if s == 0 else R("ru"))
+        mm(R("ps2", 256, 512), l0, R("e0"), True, True)
+        act(R("oh0"), R("ps2", 256, 512), Re)
+        chunk(2, "df", "cu", krow)
+        for r in range(16):
+            mm(R("ps3", 16, 32), sr(r), R("e0", r, 256, 16), r == 0, r == 15)
+        chunk(3, "df", "cu", krow)
+        if s == 0:
+            constants_3()
+        tt(R("kw", 4096, 4352), R("oh0"), nu, mul)
+        best(0)
+        if ded:
+            dd_mm(DV + DA)
+        if ded:
+            chunk(0, "df2", "du", two)
+            for c in DA:
+                dd_red(c, False)
+            chunk(1, "df2", "du", two)
+            for c in DV[:3]:
+                dd_red(c, True)
+        else:
+            gather_ahead(1, "du", 0, "ps4", "ps5")
+            chunk(0, "df2", "du", two)
+            chunk(1, "df2", "du", two, ("ps4", "ps5"))
+        best(1)
+        ts(R("bcl"), R("bi"), 2816.0, mn)
+        dd_left(R("bcl"))
+        gather_ahead(2, "du", 1024, "ps6", "ps7")
+        ts(R("w0"), R("ps3", 16, 32), 0.0, eqq, 2.0, mul)
+        tt(R("w0"), R("w0"), R("kn"), add)
+        if ded:
+            for c in DV[3:]:
+                dd_red(c, c > 4)
+        tc(R("ki", 0, 16), R("msk", 23, 264, 16))
+        tc(R("ki", 16, 32), R("cs", 15, 256, 16))
+        ts(R("kk"), R("ki"), 15, OP.bitwise_and)
+        tt(R("lb", 0, 16), R("kk", 0, 16), j16, add)
+        tt(R("lb", 16, 32), R("kk", 16, 32), j16, add)
+        tc(R("lbu"), R("lb"))
+        act(R("dbh"), IND(R("df"), R("lbu", 0, 16)), Id, bias=-0.5)
+        act(R("db"), R("dbh"), Id, bias=0.5)
+        chunk(3, "df2", "du", two)
+        chunk(2, "df2", "du", two, ("ps6", "ps7"))
+        if ded:
+            acting(t)
+        if t == 1:
+            prefix(-256.0)
+            send(s - 1, xb)
+        tt(R("sq"), IND(R("df"), R("lbu", 16, 32)), R("dbh"), add)
+        ts(R("mg"), R("sq"), 0.5, mul, MAGIC, add)
+        act(R("am"), R("mg"), Ab, bias=-MAGIC)
+        for r in range(16):
+            mm(R("ps3", 0, 16), sr(r), R("am", r, 256, 16), r == 0, False)
+        mm(R("ps3", 0, 16), wones, R("kr", 128, 144), False, True)
+        act(R("candw", 272, 528), R("mg"), Id, bias=-MAGIC)
+        ts(R("c4"), R("db"), -4.0, mx, 4.0, mn)
+        mm(R("ps2", 256, 512), ident, R("db"), True, False)
+        mm(R("ps2", 256, 512), nident, R("c4"), False, True)
+        act(R("candw", 16, 272), R("ps2", 256, 512), Cp)
+        kb, kq = R("kk", 0, 16), R("kk", 16, 32)
+        so = lambda n: R("src", 16 * n, 16 * n + 16)
+        ts(R("kh"), R("ki", 0, 16), 0x7FFFFFF0, OP.bitwise_and)
+        ts(tmp(4), kb, 16.0, mul)
+        tc(so(0), R("bi"))
+        ts(so(1), kb, 256.0, add)
+        tt(so(4), tmp(4), kq, add)
+        tt(R("ct", 0, 144), IND(R("src"), R("repc", 0, 9)), R("dft"), sub)
+        tt(R("w1"), R("kh"), R("gate", 16 * t, 16 * t + 16), mn)
+        tt(R("w1"), R("w1"), R("w0"), mn)
+        scan(R("es", 0, 128), R("rst"), R("ps0", 0, 128), BIG, mx, mn)
+        tt(R("w2"), R("w1"), R("ps3", 0, 16), mn)
+        scan(R("es", 128, 256), R("rst"), R("ps1", 0, 128), BIG, mx, mn)
+        tt(R("w3"), R("w2"), R("es", 15, 256, 16), mn)
+        ts(R("typ"), R("w3"), 7, OP.bitwise_and)
+        tt(R("mt"), IND(R("typ"), R("repu", 0, 9)), R("types"), eqq)
+        tt(R("ut"), R("mt", 0, 128), R("ct", 0, 128), mul)
+        tt(R("st1"), R("ut", 0, 64), R("ut", 64, 128), add)
+        tt(R("st"), R("st1"), R("dft", 0, 64), add)
+        tc(R("su"), R("st"))
+        fm, f3, fo = R("mt", 32, 48), R("mt", 64, 80), R("mt", 128, 144)
+        act(R("ov"), fo, Cp)
+        act(R("thr"), R("mt", 80, 112), Id, scale=1000.0, bias=-1000.0)
+        dd_right(R("su", 16, 32))
+        if t == 0:
+            tc(R("vup", 0, 16, 2), R("su", 32, 40))
+            tc(R("vup", 1, 16, 2), R("su", 40, 48))
+        tt(R("mxr"), IND(R("mxt"), R("su", 48, 64)), nu, mul)
+        if t == 1:
+            prefix_mm(R("ov"), -256.0)
+        base = tmp(5)
+        tt(base, fm, f3, add)
+        tt(R("zr"), R("mxr"), kcp, mx)
+        act(base, base, Id, scale=256.0 * s - 2304.0)
+        act(R("er"), R("zr"), Re, bias=1.0)
+        tt(R("bs", 16, 32), fm, j272, mul)
+        if t == 1:
+            prefix(-256.0)
+            send(s, xb)
+        dd_mm(DV[:5] + DA + DV[5:])
+        tt(R("bs", 0, 16), base, jd96, add)
+        if t == 1:
+            tt(R("restb"), f3, fo, add)
+            tt(R("restb"), R("restb"), R("rest"), add)
+            prefix_mm(R("restb"), 0.0)
+        for c in DA:
+            dd_red(c, False)
+        tt(R("fe"), IND(R("kw", 0, 4352), R("su", 0, 16)), R("er"), mul)
+        tt(IND(R("kw"), R("scu", 16 * t, 16 * t + 16)), R("zr"), R("fe"), add)
+        tt(R("kw", n0, n0 + 256), IND(R("knt"), R("su", 48, 64)), R("kc"), mul)
+        if s < 3:
+            head(1 - t, n0 + 256)
+        else:
+            for n in range(4):
+                act(R("yt", 704 * n, 704 * n + 704), R("kw", 704 * n, 704 * n + 704), Id, bias=4095.0)
+                dma("s", None, R("yt", 704 * n, 704 * n + 704), "out", dst=T.yc[:, 704 * n:704 * n + 704])
+        for c in DV:
+            dd_red(c, True)
+        if t == 1:
+            prefix(0.0)
+            act(R("nrx"), R("restb"), Id, scale=-1000.0, bias=1000.0)
+            tt(R("nrx"), R("nrx"), tmp(7), add)
+        tt(R("hf"), IND(R("cnt"), R("repu", 0, 2)), R("thr"), le)
+        tt(R("u3"), R("hf"), R("ct", 128, 160), mul)
+        tt(R("s3"), R("u3"), R("bs"), add)
+        tc(R("tsu"), R("s3"))
+        tt(R("av"), IND(R("candw"), R("tsu", 16, 32)), xb, add)
+        tc(IND(R("aw"), R("tsu", 0, 16)), R("av"))
+        if s < 3:
+            head_ids()
+        if t == 0:
+            act(vt, R("st", 32, 48), Cp)
+            act(R("dft", 96, 112), R("st", 32, 48), Cp)
+            tt(R("rest"), f3, fo, add)
+            act(R("ruf"), vt, Id, scale=-1.0, bias=2816.0)
+            act(R("nrest"), R("rest"), Id, scale=-1000.0)
+        elif p == 0:
+            act(vt, R("tf"), Cp)
+            act(R("dft", 96, 112), R("tf"), Cp)
+
+    def prefix_mm(src, init):
+        mm(R("ps3", 64, 80), bm, src, True, True)
+        mm(R("ps3", 48, 64), lp, src, True, init == 0.0)
+        if init:
+            mm(R("ps3", 48, 64), ident, R("njb"), False, True)
+
+    def prefix(init):
+        scan(tmp(6), tmp(1), R("ps3", 64, 80), init, mul, add)
+        tt(tmp(7), tmp(6), R("ps3", 48, 64), add)
+
+    def send(s, xb):
+        sb = lambda a, b: R("sb", 528 * s + a, 528 * s + b)
+        d = tmp(7)
+        tt(d, d, R("ov"), mul)
+        ts(sb(0, 1), R("tmp", 111, 112), 256.0, add, 48.0, mn)
+        tt(d, d, j272, add)
+        tc(R("posu"), d)
+        tc(IND(sb(0, 528), R("posu")), xb)
+        dst = T.cores[(rank + 1 + s % 7) % 8]
+        rid, pid, _se = topo.addr(dst)
+        eng = topo.engines(core, dst)
+        p, t = s // 2, s % 2
+        xw = R("xw%d" % p, 256 + 64 * t, 320 + 64 * t)
+        e["remote"](xw, sb(0, 64), "arr%d" % s, rid, pid, sum(1 << x for x in eng), len(eng))
+
+    def round_end(p):
+        xb, xw = xx(p), "xw%d" % p
+        tt(R("xdt"), IND(R("aw", 0, 4096), R("su", 32, 48)), xb, sub)
+        act(R(xw, 0, 256), R("xdt"), Ab)
+        e["landed"](R(xw, 256, 320), "arr%d" % (2 * p))
+        e["landed"](R(xw, 320, 384), "arr%d" % (2 * p + 1))
+        c0, c1, d0, cc, c0f = R(xw, 256, 257), R(xw, 320, 321), R("rg", 5, 6), R("rg", 6, 7), R("rg", 7, 8)
+        act(d0, c0, Id, scale=-1.0, bias=64.0)
+        act(c0f, c0, Cp)
+        tt(cc, c0, c1, add)
+        a, b = tmp(4), tmp(5)
+        ts(b, R("nrx"), cc, lt)
+        ts(a, R("nrx"), c0f, ge, d0, mul)
+        tt(a, a, R("nrx"), add)
+        tt(a, a, jn272, add)
+        tt(a, a, b, mul)
+        tt(a, a, jt, add)
+        tc(R("posu"), a)
+        tc(xx(p + 1), IND(R(xw), R("posu")))
+
+    head(0, 1792)
+    head_ids()
+    expand_x(xx(0))
+    thresholds()
+    step(0, 0)
+    step(0, 1)
+    round_end(0)
+    expand_x(xx(1))
+    step(1, 0)
+    step(1, 1)
+    dma("a", None, R("aw", 0, 2816), "outa", dst=T.ya[:])
+    round_end(1)
+    dma("s", None, xx(2), "out", dst=T.yx[:])
+    e["finish"]()

@@ -9,17 +9,17 @@ SHAPES = {
     "cu": (256, U), "du": (256, U), "kc": (256, F), "idp": (256, F), "y0": (256, F),
     "df": (4096, B), "df2": (4096, B), "ga": (2048, B), "e0": (256, B), "oh0": (256, B),
     "msk": (264, F), "eq": (256, F), "cn": (256, F), "zz": (256, F), "zs": (256, F), "cs": (256, F),
-    "es": (256, F), "zi": (16, I), "bi": (16, I), "bu": (16, U), "ki": (32, I), "kk": (32, I), "lb": (32, F), "lbu": (32, U),
+    "es": (256, F), "bu": (16, U), "ki": (32, I), "kk": (32, I), "lbu": (32, U),
     "kh": (16, I), "w0": (16, F), "w1": (16, F), "w2": (16, F), "w3": (16, I), "typ": (16, I),
     "dbh": (256, F), "db": (256, B), "sq": (256, F), "mg": (256, F), "am": (256, B), "c4": (256, B), "candw": (528, B),
-    "src": (96, F), "ct": (160, F), "mt": (144, F), "ut": (128, F), "st1": (64, F), "st": (64, F), "su": (64, U), "dft": (144, F),
+    "src": (112, F), "dst": (64, F), "nq": (256, F), "ct": (160, F), "mt": (144, F), "ut": (128, F), "st1": (64, F), "st": (64, F), "su": (64, U), "dft": (144, F),
     "mxr": (256, F), "zr": (256, F), "er": (256, F), "fe": (256, F),
     "codel": (256, B), "coder": (256, B), "cnt": (16, F), "aj": (256, B), "thr": (32, F), "bs": (32, F),
     "hf": (32, F), "u3": (32, F), "s3": (32, F), "tsu": (32, U), "av": (256, B), "xdt": (256, B),
     "tmp": (160, F), "ov": (16, B), "restb": (16, B), "rest": (16, F), "nrest": (16, F), "nrx": (16, F),
     "gate": (32, F), "scu": (32, U), "ruf": (16, F), "ru": (16, U), "vup": (16, U), "posu": (16, U), "bcl": (16, U),
     "kn": (16, F), "yt": (2816, F),
-    "ip": (4, I), "rg": (10, F), "k16": (16, F), "jc": (128, F), "njb": (16, B), "wide": (256, F), "wt": (1024, B), "sq1": (768, F),
+    "ip": (4, I), "rg": (10, F), "k16": (16, F), "jc": (128, F), "njb": (16, B), "wide": (256, F), "wt": (1024, B), "sq1": (896, F),
     "sr": (2064, B), "pm": (512, F), "wb": (896, B), "rst": (128, F), "rz": (128, F),
     "mxt": (288, B), "knt": (288, B), "code": (2832, B), "fl": (16, F), "constr": (256, B), "constl": (256, B),
     "rc": (16, F), "repc": (10, U), "repu": (10, U), "types": (144, F), "nu": (1024, F), "thp": (256, I), "thq": (512, I), "thb": (512, B),
@@ -196,22 +196,21 @@ def rank_program(g, core, T, topo):
 
     dma("s", R("tl"), None, "l0", src=T.tops[:])
     ms(R("thp"), 0)
+    dma("s", R("xb", 0, 256), None, "l1", src=T.x0[:])
     dma("s", R("kint", 0, 896), None, "l2", src=T.kids[:, 0:896])
     dma("a", R("kint", 896, 1792), None, "l3", src=T.kids[:, 896:1792])
-    dma("s", R("xb", 0, 256), None, "l1", src=T.x0[:])
     for n in range(8):
         dma("s", RX("thp", (slice(16 * n, 16 * n + 1), A_), 32 * n, 32 * n + 32), None, "lth", src=T.th[n:n + 1, :])
     dma("s", R("aw", 0, 896), None, "l4", src=T.a0[:, 0:896])
     dma("a", R("aw", 896, 1792), None, "l5", src=T.a0[:, 896:1792])
     ms(sq1(0), 1.0)
-    ms(R("kw", 1792, 2816), 0.0)
     ms(R("aw", 1792, 2816), 0.0)
     ms(R("sr"), 0.0)
     iota(R("ip", 0, 1), [[1, 1]], 0, 1)
     iota(R("k16"), [[1, 16]], 0, 0)
     iota(R("jc", 0, 16), [[16, 16]], 0, 0)
     iota(R("aw", 2816, 4096), [[0, 1280]], int(VOIDA), 0)
-    iota(R("kw", 2816, 4096), [[0, 1280]], 0, 0)
+    iota(R("kw", 1792, 4096), [[0, 2304]], 0, 0)
     aff(sq1(1), sq1(0), [[-1, 128]], eqq, 0.0, 0, 1)
     aff(sq1(2), sq1(0), [[-1, 128]], eqq, 0.0, 16, 1)
     aff(sq1(3), sq1(0), [[-1, 128]], eqq, 0.0, -16, 1)
@@ -221,20 +220,23 @@ def rank_program(g, core, T, topo):
     iota(R("kr", 144, 160), [[0, 16]], 3, 0)
     aff(sq1(4), sq1(0), [[-16, 8], [0, 16]], ge, 0.0, 0, 1)
     aff(sq1(4), sq1(4), [[16, 8], [0, 16]], ge, 0.0, 15, -1)
+    aff(sq1(6), sq1(4), [[-1, 128]], ge, 0.0, 0, 1)
     aff(sq1(5), sq1(4), [[1, 128]], OP.is_gt, 0.0, 0, -1)
+    aff(sq1(5), sq1(5), [[-1, 128]], OP.not_equal, -1.0, 0, 1)
     iota(R("nu", 0, 256), [[1, 256]], 1792 - 4095, 0)
-    iota(BDALL, [[0, 2048]], 0, 0)
     iota(R("wide"), [[1, 256]], 0, 0)
-    for n, v in enumerate((0, 5, 2, 1, 3, 0, 0, 4, 0)):
+    iota(R("wt", 0, 256), [[1, 16], [0, 16]], 0, 0)
+    iota(R("wt", 256, 512), [[0, 16], [1, 16]], 0, 0)
+    iota(BDALL, [[0, 2048]], 0, 0)
+    for n, v in enumerate((0, 3, 1, 4, 2, 0, 0, 6, 0)):
         iota(R("rc", n, n + 1), [[0, 1]], 16 * v, 0)
     for n, v in enumerate((2, 9, 1, 2, 3, 0, 0, 1, 5)):
         iota(R("types", 16 * n, 16 * n + 16), [[0, 16]], v, 0)
-    for n, v in enumerate((4095, 2816, None, 272, 4095, 2816, None, 272)):
-        if v:
-            iota(R("dft", 16 * n, 16 * n + 16), [[0, 16]], v, 0)
-    iota(R("src", 80, 96), [[0, 16]], 0, 0)
-    iota(R("wt", 0, 256), [[1, 16], [0, 16]], 0, 0)
-    iota(R("wt", 256, 512), [[0, 16], [1, 16]], 0, 0)
+    for n, v in ((0, 4095), (1, 2816), (4, 4095), (5, 2816)):
+        iota(R("dft", 16 * n, 16 * n + 16), [[0, 16]], v, 0)
+    for n, v in ((0, 4095), (1, 2816), (3, 272)):
+        iota(R("dst", 16 * n, 16 * n + 16), [[0, 16]], v, 0)
+    iota(R("src", 48, 64), [[0, 16]], 0, 0)
     iota(R("candw", 0, 16), [[0, 16]], 0, 0)
     for n in range(4):
         iota(R("sb", 528 * n, 528 * n + 64), [[0, 64]], 0, 0)
@@ -250,7 +252,6 @@ def rank_program(g, core, T, topo):
     tc(gf, gi)
     tc(odd, oi)
     act(even, odd, Id, bias=1.0, scale=-1.0)
-    act(bk, rf, Id, bias=4095.0, scale=4096.0)
     tc(R("tu"), R("tl"))
     tc(R("tf"), R("tl"))
     tc(R("tup", 0, 16, 2), R("tu", 0, 8))
@@ -271,22 +272,20 @@ def rank_program(g, core, T, topo):
     ms(wones, 1.0 / 128)
     ms(R("rst"), -BIG)
     ms(R("rst", 0, 128, 16), BIG)
-    ms(R("rz"), 1.0)
-    ms(R("rz", 0, 128, 16), 0.0)
     ms(R("msk", 0, 8), 0.0)
     ms(R("nrest"), 0.0)
-    jt, jd96, jd52, j16p, j272, jn272, j16, _j7 = [R("jc", 16 * n, 16 * n + 16) for n in range(8)]
+    jt, jd96, jd52, j16p, j272, jn272, j16, j16b = [R("jc", 16 * n, 16 * n + 16) for n in range(8)]
     ts(jt, jt, rf, add)
     for n, src, s in ((0, sq1(1), even), (1, sq1(2), even), (2, sq1(3), odd), (3, sq1(1), odd)):
         act(R("pm", 128 * n, 128 * n + 128), src, Id, scale=s)
-    for o, c, m in ((jd96, 4096.0, 1.0), (jd52, 4352.0, 1.0), (j16p, 16.0, 1.0), (j272, 272.0, 1.0), (jn272, 272.0, -1.0), (j16, 0.0, 16.0),
-                    (R("njb"), 0.0, -1.0), (R("src", 48, 64), 4096.0, 1.0), (R("dft", 128, 144), 4096.0, 1.0), (R("ct", 144, 160), 16.0, 1.0)):
-        act(o, jt, Id, bias=c, scale=m)
-    act(ident, sq1(1), Cp)
-    act(nident, sq1(1), Id, scale=-1.0)
-    act(m4i, sq1(1), Id, scale=-4096.0)
     ts(R("kw", 0, 896), R("kint", 0, 896), -4095.0, add)
     ts(R("kw", 896, 1792), R("kint", 896, 1792), -4095.0, add)
+
+    def lane_numbers():
+      act(nident, sq1(1), Id, scale=-1.0)
+      for o, c, m in ((jd96, 4096.0, 1.0), (jd52, 4352.0, 1.0), (j16p, 16.0, 1.0), (j272, 272.0, 1.0), (jn272, 272.0, -1.0), (j16, 0.0, 16.0), (j16b, 0.0, 16.0),
+                    (R("njb"), 0.0, -1.0), (R("src", 32, 48), 4096.0, 1.0), (R("dft", 48, 64), 16.0, 16.0), (R("dft", 112, 128), 272.0, 272.0), (R("dft", 128, 144), 4096.0, 1.0), (R("ct", 144, 160), 16.0, 1.0)):
+        act(o, jt, Id, bias=c, scale=m)
 
     def thresholds():
         ts(R("thq", 0, 256), R("thp"), 63, OP.bitwise_and)
@@ -305,13 +304,12 @@ def rank_program(g, core, T, topo):
                 act(o, xb, Cp)
 
     def constants_2():
-        tt(l0, sq1(1), sq1(5), sub)
+        act(l0, sq1(5), Id, scale=-1.0)
         act(bm, sq1(4), Cp)
-        tt(lp, sq1(5), sq1(4), sub)
+        act(lp, sq1(6), Id, scale=-1.0)
         ts(R("repu"), R("k16", 0, 10), 0.0, mul, rf, add)
-        ts(R("repc", 0, 9), R("rc", 0, 9), rf, add)
-        tc(R("dft", 32, 48), R("tf"))
-        tc(R("dft", 96, 112), R("tf"))
+        for o in (R("dft", 32, 48), R("dft", 96, 112), R("dst", 32, 48)):
+            act(o, R("tf"), Cp)
         a, b, c = R("tmp", 32, 33), R("tmp", 33, 34), R("tmp", 34, 35)
         ts(is12, rf, 12.0, eqq)
         ts(b, rf, 13.0, eqq)
@@ -331,23 +329,27 @@ def rank_program(g, core, T, topo):
         eb, ek = R("wt", 512, 768), R("wt", 768, 1024)
         ts(eb, R("wt", 0, 256), rf, eqq)
         ts(ek, R("wt", 256, 512), rf, eqq)
-        ps = R("ps3", 128, 384)
-        mm(ps, ident, eb, True, False)
-        mm(ps, ident, ek, False, True)
-        act(R("knt", 0, 256), ps, Cp)
-        mm(ps, m4i, eb, True, False)
-        mm(ps, m4i, ek, False, False)
-        mm(ps, ident, eb, False, True)
-        act(R("mxt", 0, 256), ps, Id, bias=4096.0)
+        pk, px = R("ps4", 0, 256), R("ps5", 0, 256)
+        mm(pk, ident, eb, True, False)
+        mm(pk, ident, ek, False, True)
+        mm(px, m4i, eb, True, False)
+        mm(px, m4i, ek, False, False)
+        mm(px, ident, eb, False, True)
+
+    def constants_4():
+        act(R("knt", 0, 256), R("ps4", 0, 256), Cp)
+        act(R("mxt", 0, 256), R("ps5", 0, 256), Id, bias=4096.0)
+        ts(R("repc", 0, 9), R("rc", 0, 9), rf, add)
         ms(R("knt", 256, 288), 0.0)
         ms(R("mxt", 272, 288), 4096.0)
         ts(tmp(2), R("k16"), rf, eqq)
         act(R("mxt", 256, 272), tmp(2), Id, bias=4096.0, scale=-4096.0)
+
+    def thresholds_mm():
         for h in (0, 256):
             for r in range(16):
                 mm(R("ps3", 32, 48), sr(r), R("thb", h + r, h + 256, 16), h == 0 and r == 0, False)
         mm(R("ps3", 32, 48), wones, R("kr", 144, 160), False, True)
-        act(R("kn"), R("ps3", 32, 48), Cp)
 
     def sr(r):
         return R("sr", 128 * r, 128 * r + 128)
@@ -383,7 +385,7 @@ def rank_program(g, core, T, topo):
         a, b = tmp(4), tmp(5)
         tt(b, R("dft", 32, 48), jd52, sub)
         tt(a, R("cnt"), R("nrest"), le)
-        act(R("gate", 16 * t, 16 * t + 16), a, Id, scale=1.0e6, bias=-12.0)
+        ts(R("gate", 16 * t, 16 * t + 16), a, 1.0e6, mul, -12.0, add)
         tt(b, a, b, mul)
         tt(b, b, jd52, add)
         tc(R("scu", 16 * t, 16 * t + 16), b)
@@ -404,10 +406,13 @@ def rank_program(g, core, T, topo):
         for r in range(16):
             mm(out, sr(r), RX("dx", (A_, slice(4 * q, 4 * q + 4), r, A_), 1024 * q, 1024 * q + 1024), False, r == 15)
 
+    def minus_x(q, b1, b2):
+        for h, bk2 in ((0, b1), (1, b2)):
+            mm(R(bk2), nident, RX("xe", (A_, slice(1024 * q + 512 * h, 1024 * q + 512 * h + 512)), 0, 4096), True, False)
+
     def gather_ahead(q, lst, n0, b1, b2):
         act(R("ga", n0, n0 + 1024), IND(R("aw", 0, 4096), R(lst, 64 * q, 64 * q + 64)), Cp)
         for h, bk2 in ((0, b1), (1, b2)):
-            mm(R(bk2), nident, RX("xe", (A_, slice(1024 * q + 512 * h, 1024 * q + 512 * h + 512)), 0, 4096), True, False)
             mm(R(bk2), ident, R("ga", n0 + 512 * h, n0 + 512 * h + 512), False, True)
 
     def best(h):
@@ -417,22 +422,24 @@ def rank_program(g, core, T, topo):
         m = lambda d: R("msk", 128 * h + d, 128 * h + 128 + d)
         scan(m(8), R("rst"), key, BIG, mx, mn)
         tt(w("eq"), m(8), key, eqq)
-        tt(w("cn"), m(7), key, mx)
+        tt(w("nq"), m(8), key, OP.not_equal)
         tt(w("zz"), w("eq"), R("ps2", 128 * h, 128 * h + 128), mul)
-        scan(w("zs"), R("rz"), w("zz"), 0.0, mul, mx)
-        tc(tile("zi"), R("zs", 128 * h + 15, 128 * h + 128, 16))
+        tt(w("cn"), m(7), key, mx)
+        scan(w("zs"), w("nq"), w("zz"), 0.0, mul, add)
         scan(w("cs"), w("cn"), R("rst"), BIG, mn, mx)
-        ts(tile("bi"), tile("zi"), 4095, OP.bitwise_and)
-        tc(tile("bu"), tile("bi"))
+        tc(tile("bu"), R("zs", 128 * h + 15, 128 * h + 128, 16))
         ts(w("du"), IND(R("kw", 0, 4096), tile("bu")), 4095.0, add)
 
     def head(t, n0):
         vu, vup = (R("tu"), R("tup")) if t == 0 else (R("su", 32, 48), R("vup"))
-        act(R("idp"), IND(R("kw", 0, 4096), vup), Id, bias=bk)
+        act(R("idp"), IND(R("kw", 0, 4096), vup), Id, bias=4095.0)
         ts(R("cu"), IND(R("kw", 0, 4096), vu), 4095.0, add)
         act(R("kc"), IND(R("kw", 0, 4096), vu), Cp)
-        act(R("src", 32, 48), jt, Id, bias=float(n0))
+        act(R("src", 16, 32), jt, Id, bias=float(n0))
         mm(R("ps0", 128, 384), sq1(1), R("kc"), True, True)
+        mm(R("ps1", 128, 384), sq1(1), R("nu", n0 - 1792, n0 - 1536), True, True)
+        if t == 1:
+            dd_left(vu)
 
     def head_ids():
         tr(R("y0"), R("idp"))
@@ -450,9 +457,12 @@ def rank_program(g, core, T, topo):
         ded = t == 1 or s == 0
         krow, two = R("kr", 0, 64), R("kr", 64, 128)
         kcp = R("ps0", 128, 384)
+        if not ded:
+            minus_x(1, "ps4", "ps5")
+            minus_x(2, "ps6", "ps7")
         chunk(0, "df", "cu", krow)
         if s == 0:
-            constants_2()
+            dd_left(vu)
         if t == 1:
             tt(R("ruf"), R("ruf"), R("rest"), mul)
             tt(R("ruf"), R("ruf"), vt, add)
@@ -461,17 +471,18 @@ def rank_program(g, core, T, topo):
         act(R("e0"), R("kc"), Re, bias=1.0)
         chunk(1, "df", "cu", krow)
         if ded:
-            dd_left(vu)
             dd_right(vu if s == 0 else R("ru"))
         mm(R("ps2", 256, 512), l0, R("e0"), True, True)
         act(R("oh0"), R("ps2", 256, 512), Re)
         chunk(2, "df", "cu", krow)
+        if s == 0:
+            lane_numbers()
         for r in range(16):
             mm(R("ps3", 16, 32), sr(r), R("e0", r, 256, 16), r == 0, r == 15)
         chunk(3, "df", "cu", krow)
         if s == 0:
-            constants_3()
-        tt(R("kw", 4096, 4352), R("oh0"), nu, mul)
+            act(R("kn"), R("ps3", 32, 48), Cp)
+            constants_4()
         best(0)
         if ded:
             dd_mm(DV + DA)
@@ -487,47 +498,52 @@ def rank_program(g, core, T, topo):
             chunk(0, "df2", "du", two)
             chunk(1, "df2", "du", two, ("ps4", "ps5"))
         best(1)
-        ts(R("bcl"), R("bi"), 2816.0, mn)
+        ts(R("bcl"), R("zs", 15, 256, 16), 2816.0, mn)
+        tt(R("kw", 4096, 4352), R("oh0"), R("ps1", 128, 384), mul)
         dd_left(R("bcl"))
+        if ded:
+            minus_x(2, "ps6", "ps7")
         gather_ahead(2, "du", 1024, "ps6", "ps7")
         ts(R("w0"), R("ps3", 16, 32), 0.0, eqq, 2.0, mul)
         tt(R("w0"), R("w0"), R("kn"), add)
         if ded:
-            for c in DV[3:]:
-                dd_red(c, c > 4)
+            dd_red(12, True)
+        if t == 1:
+            prefix(-256.0)
         tc(R("ki", 0, 16), R("msk", 23, 264, 16))
         tc(R("ki", 16, 32), R("cs", 15, 256, 16))
         ts(R("kk"), R("ki"), 15, OP.bitwise_and)
-        tt(R("lb", 0, 16), R("kk", 0, 16), j16, add)
-        tt(R("lb", 16, 32), R("kk", 16, 32), j16, add)
-        tc(R("lbu"), R("lb"))
+        tt(R("src", 64, 96), R("kk"), R("jc", 96, 128), add)
+        tc(R("lbu"), R("src", 64, 96))
         act(R("dbh"), IND(R("df"), R("lbu", 0, 16)), Id, bias=-0.5)
         act(R("db"), R("dbh"), Id, bias=0.5)
-        chunk(3, "df2", "du", two)
-        chunk(2, "df2", "du", two, ("ps6", "ps7"))
+        act(tmp(8), R("src", 64, 80), Id, scale=16.0)
         if ded:
-            acting(t)
-        if t == 1:
-            prefix(-256.0)
-            send(s - 1, xb)
+            for c in DV[4:]:
+                dd_red(c, False)
+        chunk(3, "df2", "du", two)
         tt(R("sq"), IND(R("df"), R("lbu", 16, 32)), R("dbh"), add)
         ts(R("mg"), R("sq"), 0.5, mul, MAGIC, add)
         act(R("am"), R("mg"), Ab, bias=-MAGIC)
         for r in range(16):
             mm(R("ps3", 0, 16), sr(r), R("am", r, 256, 16), r == 0, False)
         mm(R("ps3", 0, 16), wones, R("kr", 128, 144), False, True)
+        chunk(2, "df2", "du", two, ("ps6", "ps7"))
+        if ded:
+            acting(t)
+        if t == 1:
+            tt(tmp(9), tmp(7), R("ov"), mul)
+            ts(R("sb", 528 * s - 528, 528 * s - 527), R("tmp", 111, 112), 256.0, add, 48.0, mn)
+            ship(s - 1, xb)
         act(R("candw", 272, 528), R("mg"), Id, bias=-MAGIC)
         ts(R("c4"), R("db"), -4.0, mx, 4.0, mn)
         mm(R("ps2", 256, 512), ident, R("db"), True, False)
         mm(R("ps2", 256, 512), nident, R("c4"), False, True)
         act(R("candw", 16, 272), R("ps2", 256, 512), Cp)
-        kb, kq = R("kk", 0, 16), R("kk", 16, 32)
         so = lambda n: R("src", 16 * n, 16 * n + 16)
         ts(R("kh"), R("ki", 0, 16), 0x7FFFFFF0, OP.bitwise_and)
-        ts(tmp(4), kb, 16.0, mul)
-        tc(so(0), R("bi"))
-        ts(so(1), kb, 256.0, add)
-        tt(so(4), tmp(4), kq, add)
+        tc(so(0), R("zs", 15, 256, 16))
+        tt(so(6), tmp(8), so(5), add)
         tt(R("ct", 0, 144), IND(R("src"), R("repc", 0, 9)), R("dft"), sub)
         tt(R("w1"), R("kh"), R("gate", 16 * t, 16 * t + 16), mn)
         tt(R("w1"), R("w1"), R("w0"), mn)
@@ -539,7 +555,7 @@ def rank_program(g, core, T, topo):
         tt(R("mt"), IND(R("typ"), R("repu", 0, 9)), R("types"), eqq)
         tt(R("ut"), R("mt", 0, 128), R("ct", 0, 128), mul)
         tt(R("st1"), R("ut", 0, 64), R("ut", 64, 128), add)
-        tt(R("st"), R("st1"), R("dft", 0, 64), add)
+        tt(R("st"), R("st1"), R("dst"), add)
         tc(R("su"), R("st"))
         fm, f3, fo = R("mt", 32, 48), R("mt", 64, 80), R("mt", 128, 144)
         act(R("ov"), fo, Cp)
@@ -559,14 +575,16 @@ def rank_program(g, core, T, topo):
         tt(R("bs", 16, 32), fm, j272, mul)
         if t == 1:
             prefix(-256.0)
-            send(s, xb)
         dd_mm(DV[:5] + DA + DV[5:])
         tt(R("bs", 0, 16), base, jd96, add)
         if t == 1:
+            tt(tmp(9), tmp(7), R("ov"), mul)
+            ts(R("sb", 528 * s, 528 * s + 1), R("tmp", 111, 112), 256.0, add, 48.0, mn)
             tt(R("restb"), f3, fo, add)
             tt(R("restb"), R("restb"), R("rest"), add)
             prefix_mm(R("restb"), 0.0)
-        for c in DA:
+        hv = DV[:4] if s < 3 else DV
+        for c in DA + DV[4:] if s < 3 else ():
             dd_red(c, False)
         tt(R("fe"), IND(R("kw", 0, 4352), R("su", 0, 16)), R("er"), mul)
         tt(IND(R("kw"), R("scu", 16 * t, 16 * t + 16)), R("zr"), R("fe"), add)
@@ -577,11 +595,15 @@ def rank_program(g, core, T, topo):
             for n in range(4):
                 act(R("yt", 704 * n, 704 * n + 704), R("kw", 704 * n, 704 * n + 704), Id, bias=4095.0)
                 dma("s", None, R("yt", 704 * n, 704 * n + 704), "out", dst=T.yc[:, 704 * n:704 * n + 704])
-        for c in DV:
+            for c in DA:
+                dd_red(c, False)
+        if t == 1:
+            ship(s, xb)
+        for c in hv:
             dd_red(c, True)
         if t == 1:
             prefix(0.0)
-            act(R("nrx"), R("restb"), Id, scale=-1000.0, bias=1000.0)
+            ts(R("nrx"), R("restb"), -1000.0, mul, 1000.0, add)
             tt(R("nrx"), R("nrx"), tmp(7), add)
         tt(R("hf"), IND(R("cnt"), R("repu", 0, 2)), R("thr"), le)
         tt(R("u3"), R("hf"), R("ct", 128, 160), mul)
@@ -594,11 +616,13 @@ def rank_program(g, core, T, topo):
         if t == 0:
             act(vt, R("st", 32, 48), Cp)
             act(R("dft", 96, 112), R("st", 32, 48), Cp)
+            act(R("dst", 32, 48), R("st", 32, 48), Cp)
             tt(R("rest"), f3, fo, add)
             act(R("ruf"), vt, Id, scale=-1.0, bias=2816.0)
             act(R("nrest"), R("rest"), Id, scale=-1000.0)
         elif p == 0:
             act(vt, R("tf"), Cp)
+            act(R("dst", 32, 48), R("tf"), Cp)
             act(R("dft", 96, 112), R("tf"), Cp)
 
     def prefix_mm(src, init):
@@ -611,11 +635,9 @@ def rank_program(g, core, T, topo):
         scan(tmp(6), tmp(1), R("ps3", 64, 80), init, mul, add)
         tt(tmp(7), tmp(6), R("ps3", 48, 64), add)
 
-    def send(s, xb):
+    def ship(s, xb):
         sb = lambda a, b: R("sb", 528 * s + a, 528 * s + b)
-        d = tmp(7)
-        tt(d, d, R("ov"), mul)
-        ts(sb(0, 1), R("tmp", 111, 112), 256.0, add, 48.0, mn)
+        d = tmp(9)
         tt(d, d, j272, add)
         tc(R("posu"), d)
         tc(IND(sb(0, 528), R("posu")), xb)
@@ -647,9 +669,14 @@ def rank_program(g, core, T, topo):
         tc(xx(p + 1), IND(R(xw), R("posu")))
 
     head(0, 1792)
+    thresholds()
     head_ids()
     expand_x(xx(0))
-    thresholds()
+    act(ident, sq1(1), Cp)
+    act(m4i, sq1(1), Id, scale=-4096.0)
+    thresholds_mm()
+    constants_2()
+    constants_3()
     step(0, 0)
     step(0, 1)
     round_end(0)

from concourse.mybir import dt, AluOpType, AxisListType, ActivationFunctionType

OP = AluOpType
FN = ActivationFunctionType
F, B, I, U = "float32", "bfloat16", "int32", "uint16"
SHAPES = {
    "kint": (1792, I), "kw": (4608, F), "aw": (4352, B), "xe": (4096, B),
    "xb": (768, B), "xw0": (384, B), "xw1": (384, B), "sb": (2112, B),
    "cu": (256, U), "du": (256, U), "kc": (256, F), "idp": (256, F), "y0": (256, F),
    "df": (4096, B), "df2": (4096, B), "ga": (2048, B), "e0": (256, B), "oh0": (256, B),
    "msk": (264, F), "eq": (256, F), "cn": (256, F), "zz": (256, F), "zs": (256, F), "cs": (256, F),
    "es": (256, F), "bu": (16, U), "ki": (32, I), "kk": (32, I), "lbu": (32, U),
    "kh": (16, I), "w0": (16, F), "w1": (16, F), "w2": (16, F), "w3": (16, I), "typ": (16, I),
    "dbh": (256, F), "db": (256, B), "sq": (256, F), "mg": (256, F), "am": (256, B), "c4": (256, B), "candw": (528, B),
    "src": (112, F), "dst": (64, F), "nq": (256, F), "ct": (160, F), "mt": (144, F), "ut": (128, F), "st1": (64, F), "st": (64, F), "su": (64, U), "dft": (144, F),
    "mxr": (256, F), "zr": (256, F), "er": (256, F), "fe": (256, F),
    "codel": (256, B), "coder": (256, B), "cnt": (16, F), "aj": (256, B), "thr": (32, F), "bs": (32, F),
    "hf": (32, F), "u3": (32, F), "s3": (32, F), "tsu": (32, U), "av": (256, B), "xdt": (256, B),
    "tmp": (160, F), "ov": (16, B), "restb": (16, B), "rest": (16, F), "nrest": (16, F), "nrx": (16, F),
    "gate": (32, F), "scu": (32, U), "ruf": (16, F), "ru": (16, U), "vup": (16, U), "posu": (16, U), "bcl": (16, U),
    "kn": (16, F), "yt": (2816, F),
    "ip": (4, I), "rg": (10, F), "k16": (16, F), "jc": (128, F), "njb": (16, B), "wide": (256, F), "wt": (1024, B), "sq1": (896, F),
    "sr": (2064, B), "pm": (512, F), "wb": (896, B), "rst": (128, F), "rz": (128, F),
    "mxt": (288, B), "knt": (288, B), "code": (2832, B), "fl": (16, F), "constr": (256, B), "constl": (256, B),
    "rc": (16, F), "repc": (10, U), "repu": (10, U), "types": (144, F), "nu": (1024, F), "thp": (256, I), "thq": (512, I), "thb": (512, B),
    "tl": (16, I), "tf": (16, F), "tu": (16, U), "tup": (16, U), "kr": (160, B),
}
SCRATCH = {n: ("sbuf", [128, w], d) for n, (w, d) in SHAPES.items()}
SCRATCH["dx"] = ("sbuf", [128, 16, 16, 16], B)
SCRATCH["y4"] = ("sbuf", [128, 8, 2, 16], F)
SCRATCH["bd"] = ("sbuf", [128, 16, 128], B)
for _n in range(8):
    SCRATCH["ps%d" % _n] = ("psum", [128, 512], F)
SEMAPHORES = ["qv", "qa", "qp", "qg", "lth", "bdw", "snt", "out", "outa"] + ["l%d" % n for n in range(6)] + ["arr%d" % n for n in range(4)]
BIG = 1.0e9
MAGIC = 12582912.0
VOIDA = 16384.0
A_ = slice(None)


def R(name, lo=0, hi=None, step=1):
    hi = (SHAPES[name][0] if name in SHAPES else 512) if hi is None else hi
    return ("r", name, (A_, slice(lo, hi) if step == 1 else slice(lo, hi, step)), lo, hi)


def RX(name, idx, lo, hi):
    return ("r", name, idx, lo, hi)


def IND(win, off):
    return ("i", win, off)


def emitter(g, T):
    q = {"v": g.vector, "a": g.scalar, "p": g.tensor, "s": g.sync, "g": g}
    own = {"v": "qv", "a": "qa", "p": "qp", "g": "qg"}
    count, known, snap, wr, rd, bank = {}, {k: {} for k in q}, {}, {}, {}, {}

    def ap(x):
        if x[0] == "i":
            return T[x[1][1]][x[1][2]].indirect(T[x[2][1]][x[2][2]])
        return T[x[1]][x[2]]

    def need(k, outs, ins):
        d = {}

        def add(tag):
            d[tag[0]] = max(d.get(tag[0], 0), tag[1])
        for x in ins + outs:
            if x[1][:2] == "ps":
                for k2, tag in bank.get(x[1], {}).items():
                    if k2 != k:
                        add(tag)
        for x in ins:
            for lo, hi, tag, k2 in wr.get(x[1], []):
                if lo < x[4] and x[3] < hi and x[1][:2] != "ps":
                    add(tag)
        for x in outs:
            if x[1][:2] == "ps":
                continue
            for lst in (wr, rd):
                for lo, hi, tag, k2 in lst.get(x[1], []):
                    if lo < x[4] and x[3] < hi:
                        add(tag)
        return d

    def wait(k, d):
        for s, v in sorted(d.items(), key=lambda z: -len(snap.get(z, {}))):
            if known[k].get(s, 0) < v:
                q[k].wait_ge(T.sem[s], v)
                known[k][s] = v
                for s2, v2 in snap.get((s, v), {}).items():
                    known[k][s2] = max(known[k].get(s2, 0), v2)

    def note(k, outs, ins, tag):
        snap[tag] = dict(known[k])
        for x in outs:
            if x[1][:2] == "ps":
                bank.setdefault(x[1], {})[k] = tag
                continue
            for lst in (wr, rd):
                lst[x[1]] = [e for e in lst.get(x[1], []) if not (x[3] <= e[0] and e[1] <= x[4])]
            wr[x[1]].append((x[3], x[4], tag, k))
        for x in ins:
            if x[1][:2] == "ps":
                bank.setdefault(x[1], {})[k] = tag
                continue
            lst = [e for e in rd.get(x[1], []) if not (e[3] == k and x[3] <= e[0] and e[1] <= x[4] and e[2][0] == tag[0])]
            lst.append((x[3], x[4], tag, k))
            rd[x[1]] = lst

    def flat(xs):
        r = []
        for x in xs:
            if isinstance(x, tuple):
                r += [x[1], x[2]] if x[0] == "i" else [x]
        return r

    def op(k, call, out, ins, more=()):
        outs = [out[1]] if out[0] == "i" else [out]
        i2 = flat(ins) + ([out[2]] if out[0] == "i" else [])
        outs += flat(more)
        wait(k, need(k, outs, i2))
        s = own[k]
        count[s] = count.get(s, 0) + 1
        call().then_inc(T.sem[s], 1)
        note(k, outs, i2, (s, count[s]))

    def val(x):
        return ap(x) if isinstance(x, tuple) else x

    e = {}
    e["tt"] = lambda o, a, b, f: op("v", lambda: g.vector.tensor_tensor(ap(o), ap(a), ap(b), f), o, [a, b])

    def ts(o, a, s1, f1, s2=None, f2=None):
        if f2 is None:
            op("v", lambda: g.vector.tensor_scalar(ap(o), ap(a), val(s1), None, f1), o, [a, s1])
        else:
            op("v", lambda: g.vector.tensor_scalar(ap(o), ap(a), val(s1), val(s2), f1, f2), o, [a, s1, s2])
    e["ts"] = ts
    e["tc"] = lambda o, a: op("v", lambda: g.vector.tensor_copy(ap(o), ap(a)), o, [a])
    e["ms"] = lambda o, c: op("v", lambda: g.vector.memset(ap(o), c), o, [])
    e["scan"] = lambda o, a, b, c, f1, f2: op("v", lambda: g.vector.tensor_tensor_scan(ap(o), ap(a), ap(b), c, f1, f2), o, [a, b])
    e["tr"] = lambda o, a: op("v", lambda: g.vector.transpose(ap(o), ap(a)), o, [a])
    e["red"] = lambda o, a, f: op("v", lambda: g.vector.tensor_reduce(ap(o), ap(a), AxisListType.X, f), o, [a])

    def act(o, a, f, bias=0.0, scale=1.0, acc=None):
        if acc is not None:
            op("a", lambda: g.scalar.activation(ap(o), ap(a), f, accum_out=ap(acc)), o, [a], [acc])
        elif f == FN.Copy:
            op("a", lambda: g.scalar.activation(ap(o), ap(a), f), o, [a])
        else:
            op("a", lambda: g.scalar.activation(ap(o), ap(a), f, bias=val(bias), scale=val(scale)), o, [a, bias, scale])
    e["act"] = act
    e["mm"] = lambda o, l, r, s0, s1: op("p", lambda: g.tensor.matmul(ap(o), ap(l), ap(r), s0, s1), o, [l, r])
    e["iota"] = lambda o, pat, base, cm: op("g", lambda: g.iota(ap(o), pat, base, cm, allow_small_or_imprecise_dtypes=True), o, [])
    e["aff"] = lambda o, a, pat, f, fill, base, cm: op("g", lambda: g.affine_select(ap(o), ap(a), pat, f, fill, base, cm), o, [a])

    def dma(k, o, a, sem, src=None, dst=None):
        outs, ins = ([] if o is None else [o]), ([] if a is None else [a])
        wait(k, need("s", outs, ins))
        count[sem] = count.get(sem, 0) + 16
        q[k].dma_start(dst if o is None else ap(o), src if a is None else ap(a)).then_inc(T.sem[sem], 16)
        v = count[sem] if sem[0] == "l" and sem != "lth" else -(-count[sem] // 128) * 128
        note("s", outs, ins, (sem, v))
    e["dma"] = dma

    def remote(o, a, sem, rid, pid, mask, n):
        wait("g", need("s", [], [a]))
        count["snt"] = count.get("snt", 0) + n
        g.remote_dma(ap(o), ap(a), T.sem[sem], T.sem.snt, pid, rid, mask)
        count[sem] = n

    def landed(o, sem):
        note("s", [o], [], (sem, count[sem]))
    e["remote"], e["landed"] = remote, landed

    def finish():
        for s, v in count.items():
            q["s"].wait_ge(T.sem[s], v)
    e["finish"] = finish
    return e


def rank_program(g, core, T, topo):
    rank = T.rank_of(core)
    if rank is None:
        return
    e = emitter(g, T)
    tt, ts, tc, ms, scan, tr, red, act, mm, iota, aff, dma = [e[n] for n in ("tt", "ts", "tc", "ms", "scan", "tr", "red", "act", "mm", "iota", "aff", "dma")]
    add, sub, mul, mx, mn, eqq, lt, le, ge = OP.add, OP.subtract, OP.mult, OP.max, OP.min, OP.is_equal, OP.is_lt, OP.is_le, OP.is_ge
    Id, Cp, Ab, Re = FN.Identity, FN.Copy, FN.Abs, FN.Relu
    tmp = lambda n: R("tmp", 16 * n, 16 * n + 16)
    sq1 = lambda n: R("sq1", 128 * n, 128 * n + 128)
    BDALL = RX("bd", (A_, A_, A_), 0, 2048)

    dma("s", R("tl"), None, "l0", src=T.tops[:])
    ms(R("thp"), 0)
    dma("s", R("xb", 0, 256), None, "l1", src=T.x0[:])
    dma("s", R("kint", 0, 896), None, "l2", src=T.kids[:, 0:896])
    dma("a", R("kint", 896, 1792), None, "l3", src=T.kids[:, 896:1792])
    for n in range(8):
        dma("s", RX("thp", (slice(16 * n, 16 * n + 1), A_), 32 * n, 32 * n + 32), None, "lth", src=T.th[n:n + 1, :])
    dma("s", R("aw", 0, 896), None, "l4", src=T.a0[:, 0:896])
    dma("a", R("aw", 896, 1792), None, "l5", src=T.a0[:, 896:1792])
    ms(sq1(0), 1.0)
    ms(R("aw", 1792, 2816), 0.0)
    ms(R("sr"), 0.0)
    iota(R("ip", 0, 1), [[1, 1]], 0, 1)
    iota(R("k16"), [[1, 16]], 0, 0)
    iota(R("jc", 0, 16), [[16, 16]], 0, 0)
    iota(R("aw", 2816, 4096), [[0, 1280]], int(VOIDA), 0)
    iota(R("kw", 1792, 4096), [[0, 2304]], 0, 0)
    aff(sq1(1), sq1(0), [[-1, 128]], eqq, 0.0, 0, 1)
    aff(sq1(2), sq1(0), [[-1, 128]], eqq, 0.0, 16, 1)
    aff(sq1(3), sq1(0), [[-1, 128]], eqq, 0.0, -16, 1)
    iota(R("kr", 0, 64), [[0, 4], [1, 16]], 0, 0)
    iota(R("kr", 64, 128), [[0, 64]], 2, 0)
    iota(R("kr", 128, 144), [[0, 16]], 1, 0)
    iota(R("kr", 144, 160), [[0, 16]], 3, 0)
    aff(sq1(4), sq1(0), [[-16, 8], [0, 16]], ge, 0.0, 0, 1)
    aff(sq1(4), sq1(4), [[16, 8], [0, 16]], ge, 0.0, 15, -1)
    aff(sq1(6), sq1(4), [[-1, 128]], ge, 0.0, 0, 1)
    aff(sq1(5), sq1(4), [[1, 128]], OP.is_gt, 0.0, 0, -1)
    aff(sq1(5), sq1(5), [[-1, 128]], OP.not_equal, -1.0, 0, 1)
    iota(R("nu", 0, 256), [[1, 256]], 1792 - 4095, 0)
    iota(R("wide"), [[1, 256]], 0, 0)
    iota(R("wt", 0, 256), [[1, 16], [0, 16]], 0, 0)
    iota(R("wt", 256, 512), [[0, 16], [1, 16]], 0, 0)
    iota(BDALL, [[0, 2048]], 0, 0)
    for n, v in enumerate((0, 3, 1, 4, 2, 0, 0, 6, 0)):
        iota(R("rc", n, n + 1), [[0, 1]], 16 * v, 0)
    for n, v in enumerate((2, 9, 1, 2, 3, 0, 0, 1, 5)):
        iota(R("types", 16 * n, 16 * n + 16), [[0, 16]], v, 0)
    for n, v in ((0, 4095), (1, 2816), (4, 4095), (5, 2816)):
        iota(R("dft", 16 * n, 16 * n + 16), [[0, 16]], v, 0)
    for n, v in ((0, 4095), (1, 2816), (3, 272)):
        iota(R("dst", 16 * n, 16 * n + 16), [[0, 16]], v, 0)
    iota(R("src", 48, 64), [[0, 16]], 0, 0)
    iota(R("candw", 0, 16), [[0, 16]], 0, 0)
    for n in range(4):
        iota(R("sb", 528 * n, 528 * n + 64), [[0, 64]], 0, 0)
    for n in (1, 2, 3):
        iota(R("nu", 256 * n, 256 * n + 256), [[1, 256]], 1792 - 4095 + 256 * n, 0)

    ri, gi, oi = R("ip", 1, 2), R("ip", 2, 3), R("ip", 3, 4)
    ts(ri, R("ip", 0, 1), 15, OP.bitwise_and)
    ts(gi, R("ip", 0, 1), 4, OP.arith_shift_right)
    ts(oi, gi, 1, OP.bitwise_and)
    rf, gf, odd, even, bk, m1, m2, m3, fz, is12 = [R("rg", n, n + 1) for n in range(10)]
    tc(rf, ri)
    tc(gf, gi)
    tc(odd, oi)
    act(even, odd, Id, bias=1.0, scale=-1.0)
    tc(R("tu"), R("tl"))
    tc(R("tf"), R("tl"))
    tc(R("tup", 0, 16, 2), R("tu", 0, 8))
    tc(R("tup", 1, 16, 2), R("tu", 8, 16))
    ts(R("code", 0, 1), rf, 12.0, lt, -1.0, mul)
    ts(R("fl"), R("k16"), rf, eqq, -2.0, mul)
    act(R("fl"), R("fl"), Id, bias=1.0)
    for b in range(12):
        n, w = 1 << b, min(1 << b, 2816 - (1 << b))
        act(R("code", n, n + w), R("code", 0, w), Id, scale=R("fl", b, b + 1))
    ms(R("code", 2816, 2832), 0.0)
    b8 = R("tmp", 0, 8)
    ts(b8, R("k16", 0, 8), gf, eqq, 16.0, mul)
    ms(tmp(1), 1.0)
    for n in range(8):
        ts(RX("sr", (A_, slice(16 * n, 16 * n + 129 * 15 + 1, 129)), 0, 2064), tmp(1), R("tmp", n, n + 1), mul)
    wones, ident, nident, l0, bm, lp, m4i = [R("wb", 128 * n, 128 * n + 128) for n in range(7)]
    ms(wones, 1.0 / 128)
    ms(R("rst"), -BIG)
    ms(R("rst", 0, 128, 16), BIG)
    ms(R("msk", 0, 8), 0.0)
    ms(R("nrest"), 0.0)
    jt, jd96, jd52, j16p, j272, jn272, j16, j16b = [R("jc", 16 * n, 16 * n + 16) for n in range(8)]
    ts(jt, jt, rf, add)
    for n, src, s in ((0, sq1(1), even), (1, sq1(2), even), (2, sq1(3), odd), (3, sq1(1), odd)):
        act(R("pm", 128 * n, 128 * n + 128), src, Id, scale=s)
    ts(R("kw", 0, 896), R("kint", 0, 896), -4095.0, add)
    ts(R("kw", 896, 1792), R("kint", 896, 1792), -4095.0, add)

    def lane_numbers():
      act(nident, sq1(1), Id, scale=-1.0)
      for o, c, m in ((jd96, 4096.0, 1.0), (jd52, 4352.0, 1.0), (j16p, 16.0, 1.0), (j272, 272.0, 1.0), (jn272, 272.0, -1.0), (j16, 0.0, 16.0), (j16b, 0.0, 16.0),
                    (R("njb"), 0.0, -1.0), (R("src", 32, 48), 4096.0, 1.0), (R("dft", 48, 64), 16.0, 16.0), (R("dft", 112, 128), 272.0, 272.0), (R("dft", 128, 144), 4096.0, 1.0), (R("ct", 144, 160), 16.0, 1.0)):
        act(o, jt, Id, bias=c, scale=m)

    def thresholds():
        ts(R("thq", 0, 256), R("thp"), 63, OP.bitwise_and)
        ts(R("thq", 256, 512), R("thp"), 4032, OP.bitwise_and)
        tc(R("thb"), R("thq"))

    def xx(p):
        return R("xb", 256 * p, 256 * p + 256)

    def expand_x(xb):
        for k in range(16):
            o = RX("xe", (A_, slice(k, 4096, 16)), 256 * k, 256 * k + 256)
            if k % 3:
                tc(o, xb)
            else:
                act(o, xb, Cp)

    def constants_2():
        act(l0, sq1(5), Id, scale=-1.0)
        act(bm, sq1(4), Cp)
        act(lp, sq1(6), Id, scale=-1.0)
        ts(R("repu"), R("k16", 0, 10), 0.0, mul, rf, add)
        for o in (R("dft", 32, 48), R("dft", 96, 112), R("dst", 32, 48)):
            act(o, R("tf"), Cp)
        a, b, c = R("tmp", 32, 33), R("tmp", 33, 34), R("tmp", 34, 35)
        ts(is12, rf, 12.0, eqq)
        ts(b, rf, 13.0, eqq)
        ts(c, rf, 14.0, eqq)
        act(m1, b, Id, scale=-1.0 / 256)
        act(m2, is12, Id, scale=1.0 / 256)
        act(a, c, Id, scale=-12.0)
        tt(m2, m2, a, add)
        tt(m3, b, c, add)
        act(R("constr"), R("wide"), Id, bias=m2, scale=m1)
        act(R("constl"), R("wide"), Id, bias=m3, scale=is12)
        for n in range(8):
            p = slice(16 * n + 12, 16 * n + 16)
            dma("s", RX("bd", (p, A_, slice(16 * n, 16 * n + 16)), 256 * n, 256 * n + 256), RX("constl", (p, A_), 0, 256), "bdw")

    def constants_3():
        eb, ek = R("wt", 512, 768), R("wt", 768, 1024)
        ts(eb, R("wt", 0, 256), rf, eqq)
        ts(ek, R("wt", 256, 512), rf, eqq)
        pk, px = R("ps4", 0, 256), R("ps5", 0, 256)
        mm(pk, ident, eb, True, False)
        mm(pk, ident, ek, False, True)
        mm(px, m4i, eb, True, False)
        mm(px, m4i, ek, False, False)
        mm(px, ident, eb, False, True)

    def constants_4():
        act(R("knt", 0, 256), R("ps4", 0, 256), Cp)
        act(R("mxt", 0, 256), R("ps5", 0, 256), Id, bias=4096.0)
        ts(R("repc", 0, 9), R("rc", 0, 9), rf, add)
        ms(R("knt", 256, 288), 0.0)
        ms(R("mxt", 272, 288), 4096.0)
        ts(tmp(2), R("k16"), rf, eqq)
        act(R("mxt", 256, 272), tmp(2), Id, bias=4096.0, scale=-4096.0)

    def thresholds_mm():
        for h in (0, 256):
            for r in range(16):
                mm(R("ps3", 32, 48), sr(r), R("thb", h + r, h + 256, 16), h == 0 and r == 0, False)
        mm(R("ps3", 32, 48), wones, R("kr", 144, 160), False, True)

    def sr(r):
        return R("sr", 128 * r, 128 * r + 128)

    DB = {15: ("ps4", 0), 14: ("ps4", 256), 13: ("ps5", 0), 12: ("ps5", 224), 3: ("ps5", 432), 4: ("ps3", 256), 2: ("ps3", 336), 1: ("ps3", 384), 0: ("ps3", 416),
          11: ("ps6", 0), 10: ("ps6", 192), 7: ("ps6", 368), 9: ("ps7", 0), 8: ("ps7", 160), 6: ("ps7", 304), 5: ("ps7", 416)}
    DV, DA = (15, 14, 13, 12, 3, 4, 2, 1, 0), (11, 10, 7, 9, 8, 6, 5)

    def dd_left(lu):
        act(R("codel"), IND(R("code"), lu), Cp)
        for n in range(8):
            p = slice(16 * n, 16 * n + 12)
            dma("s", RX("bd", (p, A_, slice(16 * n, 16 * n + 16)), 256 * n, 256 * n + 256), RX("codel", (p, A_), 0, 256), "bdw")

    def dd_right(ru):
        tt(R("coder"), IND(R("code"), ru), R("constr"), add)

    def dd_out(c):
        n, o = DB[c]
        return R(n, o, o + 16 * c + 16)

    def dd_mm(cs):
        for c in cs:
            mm(dd_out(c), RX("bd", (A_, c, A_), 0, 2048), R("coder", 0, 16 * c + 16), True, True)

    def dd_red(c, v):
        if v:
            red(R("cnt", c, c + 1), dd_out(c), mx)
        else:
            act(R("aj", 0, 16 * c + 16), dd_out(c), Re, acc=R("cnt", c, c + 1))

    def acting(t):
        a, b = tmp(4), tmp(5)
        tt(b, R("dft", 32, 48), jd52, sub)
        tt(a, R("cnt"), R("nrest"), le)
        ts(R("gate", 16 * t, 16 * t + 16), a, 1.0e6, mul, -12.0, add)
        tt(b, a, b, mul)
        tt(b, b, jd52, add)
        tc(R("scu", 16 * t, 16 * t + 16), b)

    def chunk(q, dst, lst, krow, act_gather=None):
        lists = R(lst, 64 * q, 64 * q + 64)
        dxo = lambda a, b: RX("dx", (A_, slice(a, b), A_, A_), 256 * a, 256 * b)
        if act_gather:
            for h, bk2 in enumerate(act_gather):
                act(dxo(4 * q + 2 * h, 4 * q + 2 * h + 2), R(bk2), Ab)
        else:
            o = R(dst, 1024 * q, 1024 * q + 1024)
            tt(o, IND(R("aw", 0, 4096), lists), RX("xe", (A_, slice(1024 * q, 1024 * q + 1024)), 0, 4096), sub)
            act(dxo(4 * q, 4 * q + 4), o, Ab)
        n, lo = ("ps0", "ps1")[q // 2], 64 * (q % 2)
        out = R(n, lo, lo + 64)
        mm(out, wones, krow, True, False)
        for r in range(16):
            mm(out, sr(r), RX("dx", (A_, slice(4 * q, 4 * q + 4), r, A_), 1024 * q, 1024 * q + 1024), False, r == 15)

    def minus_x(q, b1, b2):
        for h, bk2 in ((0, b1), (1, b2)):
            mm(R(bk2), nident, RX("xe", (A_, slice(1024 * q + 512 * h, 1024 * q + 512 * h + 512)), 0, 4096), True, False)

    def gather_ahead(q, lst, n0, b1, b2):
        act(R("ga", n0, n0 + 1024), IND(R("aw", 0, 4096), R(lst, 64 * q, 64 * q + 64)), Cp)
        for h, bk2 in ((0, b1), (1, b2)):
            mm(R(bk2), ident, R("ga", n0 + 512 * h, n0 + 512 * h + 512), False, True)

    def best(h):
        key = R(("ps0", "ps1")[h], 0, 128)
        w = lambda n: R(n, 128 * h, 128 * h + 128)
        tile = lambda n: R(n, 8 * h, 8 * h + 8)
        m = lambda d: R("msk", 128 * h + d, 128 * h + 128 + d)
        scan(m(8), R("rst"), key, BIG, mx, mn)
        tt(w("eq"), m(8), key, eqq)
        tt(w("nq"), m(8), key, OP.not_equal)
        tt(w("zz"), w("eq"), R("ps2", 128 * h, 128 * h + 128), mul)
        tt(w("cn"), m(7), key, mx)
        scan(w("zs"), w("nq"), w("zz"), 0.0, mul, add)
        scan(w("cs"), w("cn"), R("rst"), BIG, mn, mx)
        tc(tile("bu"), R("zs", 128 * h + 15, 128 * h + 128, 16))
        ts(w("du"), IND(R("kw", 0, 4096), tile("bu")), 4095.0, add)

    def head(t, n0):
        vu, vup = (R("tu"), R("tup")) if t == 0 else (R("su", 32, 48), R("vup"))
        act(R("idp"), IND(R("kw", 0, 4096), vup), Id, bias=4095.0)
        ts(R("cu"), IND(R("kw", 0, 4096), vu), 4095.0, add)
        act(R("kc"), IND(R("kw", 0, 4096), vu), Cp)
        act(R("src", 16, 32), jt, Id, bias=float(n0))
        mm(R("ps0", 128, 384), sq1(1), R("kc"), True, True)
        mm(R("ps1", 128, 384), sq1(1), R("nu", n0 - 1792, n0 - 1536), True, True)
        if t == 1:
            dd_left(vu)

    def head_ids():
        tr(R("y0"), R("idp"))
        act(RX("y4", (A_, A_, A_, A_), 0, 256), R("y0"), Cp)
        for cc in (0, 1):
            for gg in (0, 1):
                mm(R("ps2", 128 * cc, 128 * cc + 128), R("pm", 256 * cc + 128 * gg, 256 * cc + 128 * gg + 128), RX("y4", (A_, A_, gg, A_), 0, 256), gg == 0, gg == 1)

    def step(p, t):
        s = 2 * p + t
        xb, vt = xx(p), R("dft", 32, 48)
        vu = R("tu") if t == 0 else R("su", 32, 48)
        n0 = 1792 + 256 * s
        nu = R("nu", 256 * s, 256 * s + 256)
        ded = t == 1 or s == 0
        krow, two = R("kr", 0, 64), R("kr", 64, 128)
        kcp = R("ps0", 128, 384)
        if not ded:
            minus_x(1, "ps4", "ps5")
            minus_x(2, "ps6", "ps7")
        chunk(0, "df", "cu", krow)
        if s == 0:
            dd_left(vu)
        if t == 1:
            tt(R("ruf"), R("ruf"), R("rest"), mul)
            tt(R("ruf"), R("ruf"), vt, add)
            tc(R("ru"), R("ruf"))
            prefix_mm(R("ov"), -256.0)
        act(R("e0"), R("kc"), Re, bias=1.0)
        chunk(1, "df", "cu", krow)
        if ded:
            dd_right(vu if s == 0 else R("ru"))
        mm(R("ps2", 256, 512), l0, R("e0"), True, True)
        act(R("oh0"), R("ps2", 256, 512), Re)
        chunk(2, "df", "cu", krow)
        if s == 0:
            lane_numbers()
        for r in range(16):
            mm(R("ps3", 16, 32), sr(r), R("e0", r, 256, 16), r == 0, r == 15)
        chunk(3, "df", "cu", krow)
        if s == 0:
            act(R("kn"), R("ps3", 32, 48), Cp)
            constants_4()
        best(0)
        if ded:
            dd_mm(DV + DA)
        if ded:
            chunk(0, "df2", "du", two)
            for c in DA:
                dd_red(c, False)
            chunk(1, "df2", "du", two)
            for c in DV[:3]:
                dd_red(c, True)
        else:
            gather_ahead(1, "du", 0, "ps4", "ps5")
            chunk(0, "df2", "du", two)
            chunk(1, "df2", "du", two, ("ps4", "ps5"))
        best(1)
        ts(R("bcl"), R("zs", 15, 256, 16), 2816.0, mn)
        tt(R("kw", 4096, 4352), R("oh0"), R("ps1", 128, 384), mul)
        dd_left(R("bcl"))
        if ded:
            minus_x(2, "ps6", "ps7")
        gather_ahead(2, "du", 1024, "ps6", "ps7")
        ts(R("w0"), R("ps3", 16, 32), 0.0, eqq, 2.0, mul)
        tt(R("w0"), R("w0"), R("kn"), add)
        if ded:
            dd_red(12, True)
        if t == 1:
            prefix(-256.0)
        tc(R("ki", 0, 16), R("msk", 23, 264, 16))
        tc(R("ki", 16, 32), R("cs", 15, 256, 16))
        ts(R("kk"), R("ki"), 15, OP.bitwise_and)
        tt(R("src", 64, 96), R("kk"), R("jc", 96, 128), add)
        tc(R("lbu"), R("src", 64, 96))
        act(R("dbh"), IND(R("df"), R("lbu", 0, 16)), Id, bias=-0.5)
        act(R("db"), R("dbh"), Id, bias=0.5)
        act(tmp(8), R("src", 64, 80), Id, scale=16.0)
        if ded:
            for c in DV[4:]:
                dd_red(c, False)
        chunk(3, "df2", "du", two)
        tt(R("sq"), IND(R("df"), R("lbu", 16, 32)), R("dbh"), add)
        ts(R("mg"), R("sq"), 0.5, mul, MAGIC, add)
        act(R("am"), R("mg"), Ab, bias=-MAGIC)
        for r in range(16):
            mm(R("ps3", 0, 16), sr(r), R("am", r, 256, 16), r == 0, False)
        mm(R("ps3", 0, 16), wones, R("kr", 128, 144), False, True)
        chunk(2, "df2", "du", two, ("ps6", "ps7"))
        if ded:
            acting(t)
        if t == 1:
            tt(tmp(9), tmp(7), R("ov"), mul)
            ts(R("sb", 528 * s - 528, 528 * s - 527), R("tmp", 111, 112), 256.0, add, 48.0, mn)
            ship(s - 1, xb)
        act(R("candw", 272, 528), R("mg"), Id, bias=-MAGIC)
        ts(R("c4"), R("db"), -4.0, mx, 4.0, mn)
        mm(R("ps2", 256, 512), ident, R("db"), True, False)
        mm(R("ps2", 256, 512), nident, R("c4"), False, True)
        act(R("candw", 16, 272), R("ps2", 256, 512), Cp)
        so = lambda n: R("src", 16 * n, 16 * n + 16)
        ts(R("kh"), R("ki", 0, 16), 0x7FFFFFF0, OP.bitwise_and)
        tc(so(0), R("zs", 15, 256, 16))
        tt(so(6), tmp(8), so(5), add)
        tt(R("ct", 0, 144), IND(R("src"), R("repc", 0, 9)), R("dft"), sub)
        tt(R("w1"), R("kh"), R("gate", 16 * t, 16 * t + 16), mn)
        tt(R("w1"), R("w1"), R("w0"), mn)
        scan(R("es", 0, 128), R("rst"), R("ps0", 0, 128), BIG, mx, mn)
        tt(R("w2"), R("w1"), R("ps3", 0, 16), mn)
        scan(R("es", 128, 256), R("rst"), R("ps1", 0, 128), BIG, mx, mn)
        tt(R("w3"), R("w2"), R("es", 15, 256, 16), mn)
        ts(R("typ"), R("w3"), 7, OP.bitwise_and)
        tt(R("mt"), IND(R("typ"), R("repu", 0, 9)), R("types"), eqq)
        tt(R("ut"), R("mt", 0, 128), R("ct", 0, 128), mul)
        tt(R("st1"), R("ut", 0, 64), R("ut", 64, 128), add)
        tt(R("st"), R("st1"), R("dst"), add)
        tc(R("su"), R("st"))
        fm, f3, fo = R("mt", 32, 48), R("mt", 64, 80), R("mt", 128, 144)
        act(R("ov"), fo, Cp)
        act(R("thr"), R("mt", 80, 112), Id, scale=1000.0, bias=-1000.0)
        dd_right(R("su", 16, 32))
        if t == 0:
            tc(R("vup", 0, 16, 2), R("su", 32, 40))
            tc(R("vup", 1, 16, 2), R("su", 40, 48))
        tt(R("mxr"), IND(R("mxt"), R("su", 48, 64)), nu, mul)
        if t == 1:
            prefix_mm(R("ov"), -256.0)
        base = tmp(5)
        tt(base, fm, f3, add)
        tt(R("zr"), R("mxr"), kcp, mx)
        act(base, base, Id, scale=256.0 * s - 2304.0)
        act(R("er"), R("zr"), Re, bias=1.0)
        tt(R("bs", 16, 32), fm, j272, mul)
        if t == 1:
            prefix(-256.0)
        dd_mm(DV[:5] + DA + DV[5:])
        tt(R("bs", 0, 16), base, jd96, add)
        if t == 1:
            tt(tmp(9), tmp(7), R("ov"), mul)
            ts(R("sb", 528 * s, 528 * s + 1), R("tmp", 111, 112), 256.0, add, 48.0, mn)
            tt(R("restb"), f3, fo, add)
            tt(R("restb"), R("restb"), R("rest"), add)
            prefix_mm(R("restb"), 0.0)
        hv = DV[:4] if s < 3 else DV
        for c in DA + DV[4:] if s < 3 else ():
            dd_red(c, False)
        tt(R("fe"), IND(R("kw", 0, 4352), R("su", 0, 16)), R("er"), mul)
        tt(IND(R("kw"), R("scu", 16 * t, 16 * t + 16)), R("zr"), R("fe"), add)
        tt(R("kw", n0, n0 + 256), IND(R("knt"), R("su", 48, 64)), R("kc"), mul)
        if s < 3:
            head(1 - t, n0 + 256)
        else:
            for n in range(4):
                act(R("yt", 704 * n, 704 * n + 704), R("kw", 704 * n, 704 * n + 704), Id, bias=4095.0)
                dma("s", None, R("yt", 704 * n, 704 * n + 704), "out", dst=T.yc[:, 704 * n:704 * n + 704])
            for c in DA:
                dd_red(c, False)
        if t == 1:
            ship(s, xb)
        for c in hv:
            dd_red(c, True)
        if t == 1:
            prefix(0.0)
            ts(R("nrx"), R("restb"), -1000.0, mul, 1000.0, add)
            tt(R("nrx"), R("nrx"), tmp(7), add)
        tt(R("hf"), IND(R("cnt"), R("repu", 0, 2)), R("thr"), le)
        tt(R("u3"), R("hf"), R("ct", 128, 160), mul)
        tt(R("s3"), R("u3"), R("bs"), add)
        tc(R("tsu"), R("s3"))
        tt(R("av"), IND(R("candw"), R("tsu", 16, 32)), xb, add)
        tc(IND(R("aw"), R("tsu", 0, 16)), R("av"))
        if s < 3:
            head_ids()
        if t == 0:
            act(vt, R("st", 32, 48), Cp)
            act(R("dft", 96, 112), R("st", 32, 48), Cp)
            act(R("dst", 32, 48), R("st", 32, 48), Cp)
            tt(R("rest"), f3, fo, add)
            act(R("ruf"), vt, Id, scale=-1.0, bias=2816.0)
            act(R("nrest"), R("rest"), Id, scale=-1000.0)
        elif p == 0:
            act(vt, R("tf"), Cp)
            act(R("dst", 32, 48), R("tf"), Cp)
            act(R("dft", 96, 112), R("tf"), Cp)

    def prefix_mm(src, init):
        mm(R("ps3", 64, 80), bm, src, True, True)
        mm(R("ps3", 48, 64), lp, src, True, init == 0.0)
        if init:
            mm(R("ps3", 48, 64), ident, R("njb"), False, True)

    def prefix(init):
        scan(tmp(6), tmp(1), R("ps3", 64, 80), init, mul, add)
        tt(tmp(7), tmp(6), R("ps3", 48, 64), add)

    def ship(s, xb):
        sb = lambda a, b: R("sb", 528 * s + a, 528 * s + b)
        d = tmp(9)
        tt(d, d, j272, add)
        tc(R("posu"), d)
        tc(IND(sb(0, 528), R("posu")), xb)
        dst = T.cores[(rank + 1 + s % 7) % 8]
        rid, pid, _se = topo.addr(dst)
        eng = topo.engines(core, dst)
        p, t = s // 2, s % 2
        xw = R("xw%d" % p, 256 + 64 * t, 320 + 64 * t)
        e["remote"](xw, sb(0, 64), "arr%d" % s, rid, pid, sum(1 << x for x in eng), len(eng))

    def round_end(p):
        xb, xw = xx(p), "xw%d" % p
        tt(R("xdt"), IND(R("aw", 0, 4096), R("su", 32, 48)), xb, sub)
        act(R(xw, 0, 256), R("xdt"), Ab)
        e["landed"](R(xw, 256, 320), "arr%d" % (2 * p))
        e["landed"](R(xw, 320, 384), "arr%d" % (2 * p + 1))
        c0, c1, d0, cc, c0f = R(xw, 256, 257), R(xw, 320, 321), R("rg", 5, 6), R("rg", 6, 7), R("rg", 7, 8)
        act(d0, c0, Id, scale=-1.0, bias=64.0)
        act(c0f, c0, Cp)
        tt(cc, c0, c1, add)
        a, b = tmp(4), tmp(5)
        ts(b, R("nrx"), cc, lt)
        ts(a, R("nrx"), c0f, ge, d0, mul)
        tt(a, a, R("nrx"), add)
        tt(a, a, jn272, add)
        tt(a, a, b, mul)
        tt(a, a, jt, add)
        tc(R("posu"), a)
        tc(xx(p + 1), IND(R(xw), R("posu")))

    head(0, 1792)
    thresholds()
    head_ids()
    expand_x(xx(0))
    act(ident, sq1(1), Cp)
    act(m4i, sq1(1), Id, scale=-4096.0)
    thresholds_mm()
    constants_2()
    constants_3()
    step(0, 0)
    step(0, 1)
    round_end(0)
    expand_x(xx(1))
    step(1, 0)
    step(1, 1)
    dma("a", None, R("aw", 0, 2816), "outa", dst=T.ya[:])
    round_end(1)
    dma("s", None, xx(2), "out", dst=T.yx[:])
    e["finish"]()
